import numpy as np, ml_dtypes
CORES = [3,7,11,15,131,135,139,143]
N = 8
BF = ml_dtypes.bfloat16
W, V, Q, S, RO = 2048, 256, 4, 5, 3
RK = np.arange(N)[:, None, None]; GR = np.arange(8)[None, :, None]; VE = np.arange(V)[None, None, :]
def unfold(a, m):
    return np.ascontiguousarray(a.reshape(N, 8, 16, m).transpose(0, 1, 3, 2))
def fold(a):
    return np.ascontiguousarray(a.transpose(0, 1, 3, 2)).reshape(N, 128, -1)
def pack(T, U, P, x):
    return {"tx": fold(T).astype(np.float32).astype(BF), "pu": fold(U).astype(np.int32), "p0": fold(P).astype(np.int32), "x0": fold(x).astype(np.float32).astype(BF)}
def pair(rng, P):
    m = rng.integers(0, 17, (N, 8, V // 2, 1))
    P[:, :, 1::2] = np.where(np.arange(16) < m, P[:, :, 0::2], P[:, :, 1::2])
    return P
def parts(rng):
    T = rng.integers(0, 128, (N, 8, W, 16)); U = rng.integers(0, W, (N, 8, W, 16))
    U = np.where(rng.random((N, 8, W, 1)) < 0.25, U[..., :1], U)
    P = rng.integers(0, W, (N, 8, V, 16))
    for k in range(1, 16):
        nxt = U[RK, GR, P[..., k - 1], rng.integers(0, 16, (N, 8, V))]
        P[..., k] = np.where(rng.random((N, 8, V)) < 0.5, nxt, P[..., k])
    P = pair(rng, P)
    near = np.clip(T[RK, GR, P[..., 15]] + rng.integers(-20, 21, (N, 8, V, 16)), 0, 127)
    x = np.where(rng.random((N, 8, V, 1)) < 0.5, near, rng.integers(0, 128, (N, 8, V, 16)))
    return T, U, P, x
def setup_inputs(rng):
    return pack(*parts(rng))
def setup_inputs_ties(rng):
    T, U, P, x = parts(rng)
    few = rng.integers(0, 128, (N, 8, 6, 16)); few[:, :, 0] = 0; few[:, :, 1] = 127
    T = few[RK, GR, rng.integers(0, 6, (N, 8, W))]; x = few[RK, GR, rng.integers(0, 6, (N, 8, V))]
    return pack(T, U, P, x)
def setup_inputs_cuts(rng):
    T, U, P, x = parts(rng); h = W // 2; s = V // 4
    for g in range(8):
        o = rng.permutation(W); P[:, g] = o[h + P[:, g] % h]
        for j in range(s):
            m = (1, Q - 1, Q, N)[j if j < 4 else int(rng.integers(0, 4))]
            nm = o[s + np.arange(N)]; nm[rng.permutation(N)[:m]] = o[j]
            P[:, g, 2 * j + 1] = P[:, g, 2 * j]; P[:, g, 2 * j:2 * j + 2, 15] = nm[:, None]
    return pack(T, U, P, x)
def setup_inputs_crowd(rng):
    T, U, P, x = parts(rng); h = V // 2; r = np.arange(N)[:, None]; j = np.arange(h)[None, :]
    for g in (0, 1, 2, 3, 4, 5, 7):
        o = rng.permutation(W); nm = np.repeat(o[1:N + 1, None], V, axis=1); n = N + 1
        if g in (0, 7):
            if g == 7: o = np.concatenate([np.array([W - 1]), rng.permutation(W - 1)])
            nm = np.stack([rng.permutation(o[i * V:(i + 1) * V]) for i in np.minimum(rng.permutation(N) // Q, N // Q - 1)]); n = (N // Q) * V
        elif g in (1, 4):
            o = 1 + rng.permutation(W - 1); n = ((N - 1) // (Q - 1) + 1) * h
            nm = o[(rng.permutation(N) // (Q - 1))[:, None] * h + np.arange(V)[None, :] // 2]
        elif g == 2: nm[rng.permutation(N)[:Q]] = o[0]
        elif g == 5:
            s = int(rng.integers(0, N - Q + 1)); nm[s:s + Q - 1, :192] = o[0]; nm = nm[:, rng.permutation(V)]
        else: o = np.arange(W)[::-1]; n = 512
        a, b = o[:n], o[n:]
        T[:, g] = T[:, g] >> 2; x[:, g] = x[:, g] >> 2; T[:, g, a] = T[:, g, a] + 96
        P[:, g] = b[P[:, g] % len(b)]; U[:, g] = b[U[:, g] % len(b)]; P[:, g, 1::2] = np.array(P[:, g, 0::2])
        if g == 3:
            m = rng.integers(1, 15, (N, h)); c = W - 512 + 4 * rng.integers(0, 128, (N, h))
            P[r, g, 2 * j, m] = c; P[r, g, 2 * j + 1, m] = c + 1
        else: P[:, g, :, 15] = nm
        if g in (0, 7): P[:, g, :, 14] = np.array(P[:1, g, :, 14]); U[:, g] = np.array(U[:1, g, :, :1])
    return pack(T, U, P, x)
def setup_inputs_few(rng):
    T, U, P, x = parts(rng)
    for g in (0, 2, 4, 6):
        a = np.concatenate([np.array([0, W - 1]), rng.integers(0, W, 10)]); P[:, g] = a[P[:, g] % 12]
        if g in (0, 4): U[:, g] = a[U[:, g] % 12]
    P[:, 2] = np.array(P[:, 2, :, :1]); U[:, 4, ::2] = rng.integers(0, W, (N, W // 2, 16)); U[:, 6] = np.arange(W)[:, None]
    return pack(T, U, P, x)
def setup_inputs_spread(rng):
    T = np.minimum((np.exp2(7 * rng.random((N, 8, W, 1))) * rng.random((N, 8, W, 16))).astype(np.int64), 127)
    x = np.minimum((np.exp2(7 * rng.random((N, 8, V, 1))) * rng.random((N, 8, V, 16))).astype(np.int64), 127)
    U = np.minimum((W * rng.random((N, 8, W, 16)) ** 2).astype(np.int64), W - 1)
    P = np.minimum((W * rng.random((N, 8, V, 16)) ** 3).astype(np.int64), W - 1)
    return pack(T, U, pair(rng, P), x)
def check_inputs(d):
    bad = []
    for k, hi in (("tx", 127), ("pu", W - 1), ("p0", W - 1), ("x0", 127)):
        a = np.asarray(d[k]).astype(np.float64)
        if not (np.all(a >= 0) and np.all(a <= hi)): bad.append("range of " + k)
        elif np.any(np.floor(a) != a): bad.append("whole numbers of " + k)
    return bad
def reference(tx, pu, p0, x0):
    T = unfold(tx.astype(np.float32).astype(np.int32), W); U = unfold(pu.astype(np.int64), W)
    P = unfold(p0.astype(np.int64), V); x = unfold(x0.astype(np.float32).astype(np.int32), V)
    row = np.arange(16); cut = np.zeros((8, W), bool); R4 = RK[..., None]; G4 = GR[..., None]
    for rnd in range(RO):
        d = np.add.reduce(np.abs(T[R4, G4, P] - x[:, :, :, None, :]), axis=4)
        differ = P != P[:, :, np.arange(V) ^ 1]
        q = np.where(np.any(differ, axis=3), np.argmax(differ, axis=3), 15)
        f = np.argmax(np.where(row >= np.maximum(q, 1)[..., None], d, -1), axis=3)
        old = cut[G4, P] & (row >= 1)
        k = np.where(np.any(old, axis=3), np.argmax(old, axis=3), f)
        charged = np.zeros((N, 8, W), bool); charged[RK, GR, P[RK, GR, VE, f]] = True
        cut = cut | (np.add.reduce(charged.astype(np.int64), axis=0) >= Q)
        T[:, cut] = 256
        pup = U[RK, GR, P[RK, GR, VE, k - 1]]
        e = np.add.reduce(np.abs(T[R4, G4, pup] - x[:, :, :, None, :]), axis=4)
        b = np.argmin(e, axis=3); best = pup[RK, GR, VE, b]
        take = e[RK, GR, VE, b] < d[RK, GR, VE, k]
        P[RK, GR, VE, k] = np.where(take, best, P[RK, GR, VE, k])
        x = np.where(take[..., None], (x + T[RK, GR, best]) >> 1, x)
        if rnd + 1 < RO: P = np.roll(P, S, axis=0); x = np.roll(x, S, axis=0)
    return {"yp": fold(P).astype(np.float32), "yx": fold(x).astype(np.float32).astype(BF), "yc": np.repeat(cut[None], N, axis=0).astype(np.float32)}

@@ -1,0 +1,466 @@
+from concourse.bass import DstId, RemoteDMATransfer
+from concourse.mybir import dt, AluOpType as OP, ActivationFunctionType as AF
+
+NR = 3
+STEP = 5
+NG = 8
+BIG = 262144.0
+
+F4, BF, HF, I4, U2 = "float32", "bfloat16", "float16", "int32", "uint16"
+SCRATCH = {}
+for _n, _w, _d in (
+        ("TXR", 2048, BF), ("TX", 2304, BF), ("PU", 2048, I4), ("P0R", 256, I4), ("X0R", 256, BF),
+        ("XR", 1024, BF), ("DF", 4096, BF), ("AD", 4096, BF), ("TG", 512, BF), ("OU", 2048, BF), ("OV", 2048, BF),
+        ("PI", 8, I4), ("PF", 12, F4), ("IF", 144, F4), ("MU", 128, F4), ("MG", 128, F4), ("FS", 144, BF), ("ID", 128, BF), ("NID", 128, BF),
+        ("SW", 512, HF), ("ONB", 128, BF), ("ONF", 256, F4), ("NEGC", 128, F4), ("BGC", 256, F4), ("REP", 2048, BF), ("BD", 128, BF),
+        ("H16", 16, F4), ("IU", 128, BF), ("IV", 128, BF), ("BDM", 128, F4), ("KREV", 256, F4), ("KFW", 128, BF), ("KRV0", 128, F4),
+        ("NEGM", 128, F4), ("RES", 256, F4), ("RES1", 256, F4), ("RESB", 256, F4), ("BIGK", 256, F4), ("BASE", 16, F4), ("BKA", 256, F4), ("BKB", 256, F4),
+        ("A16", 256, HF), ("PFL", 256, F4), ("FM", 256, F4), ("RR", 256, F4), ("D1", 256, F4), ("LT", 256, F4), ("PAYI", 16, I4), ("UVI", 32, I4),
+        ("UVF", 32, F4), ("TEI", 16, I4), ("TEO", 16, U2), ("PKI", 16, I4), ("PK", 16, F4), ("DKM", 16, F4), ("DKI", 16, I4), ("DKJ", 16, I4),
+        ("PZ", 256, F4), ("THA", 128, F4), ("THB", 256, F4), ("T1", 256, F4), ("PDO", 256, U2), ("CUT", 128, BF),
+        ("CAC", 128, F4), ("CA2", 128, F4), ("TK", 16, F4), ("O1", 16, F4), ("O2", 16, F4), ("OF", 16, F4), ("OFO", 16, U2),
+        ("N1", 16, F4), ("N2", 16, F4), ("SU", 256, F4), ("EQ", 128, F4), ("PRE", 128, F4), ("PM", 128, F4), ("TA", 256, F4), ("TB", 256, F4),
+        ("YPA", 256, F4), ("YPB", 256, F4), ("YXB", 256, BF)):
+    SCRATCH[_n] = ("sbuf", [128, _w], _d)
+SCRATCH["XQ"] = ("sbuf", [128, 16, 4, 16], BF)
+for _n in ("C16", "PNH"):
+    SCRATCH[_n] = ("sbuf", [128, 16, 16], HF)
+SCRATCH["sps"] = ("psum", [128, 32, 16], F4)
+for _n in ("dps", "eps", "kps", "t0", "t1", "t2", "t3"):
+    SCRATCH[_n] = ("psum", [128, 512], F4)
+for _r in range(NR):
+    SCRATCH["Y%d" % _r] = ("sbuf", [128, 256], BF)
+    SCRATCH["YS%d" % (_r + 1)] = ("sbuf", [128, 256], BF)
+    for _s in ("", "S") if _r else ("",):
+        SCRATCH["PO%s%d" % (_s, _r)] = ("sbuf", [128, 256], U2)
+        SCRATCH["KM%s%d" % (_s, _r)] = ("sbuf", [128, 128], BF)
+        SCRATCH["PA%s%d" % (_s, _r)] = ("sbuf", [128, 256], F4)
+    SCRATCH["MK%d" % _r] = ("sbuf", [128, 1024], BF)
+    SCRATCH["MS%d" % _r] = ("sbuf", [128, 128], BF)
+PSUM = [n for n in SCRATCH if SCRATCH[n][0] == "psum"]
+
+LOADS = ["lp0", "lx0", "ltx0", "ltx1", "ltx2", "ltx3", "lpu0", "lpu1"]
+SEMAPHORES = (["qv", "qs", "qp", "qg", "loc", "oyp", "oyx", "oyc"] + LOADS + ["mk%d_%d" % (r, j) for r in range(NR) for j in range(NG)]
+              + ["%s_%d" % (n, r) for r in range(1, NR) for n in ("ry", "rp", "rk", "ra")])
+
+
+def rank_program(g, core, T, topo):
+    rank = T.rank_of(core)
+    if rank is None:
+        return
+    Q = {"V": g.vector, "S": g.scalar, "P": g.tensor, "G": g, "Y": g.sync}
+    SEM = {"V": "qv", "S": "qs", "P": "qp", "G": "qg"}
+    cnt = {"V": 0, "S": 0, "P": 0, "G": 0}
+    known = {q: {} for q in Q}
+    acc = {}
+    sent = [0]
+
+    def A(n, lo=0, hi=None, st=1):
+        hi = SCRATCH[n][1][1] if hi is None else hi
+        return (T[n][:, lo:hi] if st == 1 else T[n][:, lo:hi:st], n, lo, hi)
+
+    def B(ap, n, lo, hi):
+        return (ap, n, lo, hi)
+
+    def need(q, ins, outs):
+        w = {}
+        for isw, ops in ((False, ins), (True, outs)):
+            for (_, n, lo, hi) in ops:
+                for (l2, h2, w2, q2, s2, v2) in acc.get(n, ()):
+                    ps = n in PSUM
+                    if ps and q2 == q and q == "P":
+                        continue
+                    hit = ps and q2 != q
+                    hit = hit or ((isw or w2) and lo < h2 and l2 < hi)
+                    if hit and known[q].get(s2, 0) < v2:
+                        w[s2] = max(w.get(s2, 0), v2)
+        for s in sorted(w):
+            Q[q].wait_ge(T.sem[s], w[s])
+            known[q][s] = w[s]
+
+    def note(q, s, v, ins, outs):
+        for (_, n, lo, hi) in outs:
+            acc[n] = [e for e in acc.get(n, []) if (e[3] == q or n not in PSUM) and not (lo <= e[0] and e[1] <= hi)]
+            acc[n].append((lo, hi, True, q, s, v))
+        for (_, n, lo, hi) in ins:
+            acc.setdefault(n, []).append((lo, hi, False, q, s, v))
+
+    def do(q, f, outs, ins):
+        need(q, ins, outs)
+        f().then_inc(T.sem[SEM[q]], 1)
+        cnt[q] += 1
+        note(q, SEM[q], cnt[q], ins, outs)
+
+    def cp(o, i):
+        do("V", lambda: g.vector.tensor_copy(o[0], i[0]), [o], [i])
+
+    def tt(o, a, b, op):
+        do("V", lambda: g.vector.tensor_tensor(o[0], a[0], b[0], op), [o], [a, b])
+
+    def ts(o, a, s1, op0, s2=None, op1=None):
+        extra = [s for s in (s1, s2) if isinstance(s, tuple)]
+        v1 = s1[0] if isinstance(s1, tuple) else s1
+        v2 = s2[0] if isinstance(s2, tuple) else s2
+        if op1 is None:
+            do("V", lambda: g.vector.tensor_scalar(o[0], a[0], v1, None, op0), [o], [a] + extra)
+        else:
+            do("V", lambda: g.vector.tensor_scalar(o[0], a[0], v1, v2, op0, op1), [o], [a] + extra)
+
+    def scan(o, d0, d1, op0, op1):
+        do("V", lambda: g.vector.tensor_tensor_scan(o[0], d0[0], d1[0], 0.0, op0, op1), [o], [d0, d1])
+
+    def t32(o, i):
+        do("V", lambda: g.vector.transpose(o[0], i[0]), [o], [i])
+
+    def gat(o, win, off, in1=None, op=None):
+        ap = win[0].indirect(off[0])
+        if in1 is None:
+            do("V", lambda: g.vector.tensor_copy(o[0], ap), [o], [win, off])
+        else:
+            do("V", lambda: g.vector.tensor_tensor(o[0], ap, in1[0], op), [o], [win, off, in1])
+
+    def act(o, i, func=AF.Identity, scale=1.0, bias=0.0):
+        do("S", lambda: g.scalar.activation(o[0], i[0], func, bias=bias, scale=scale), [o], [i])
+
+    def mm(o, l, r, start, stop):
+        do("P", lambda: g.tensor.matmul(o[0], l[0], r[0], start, stop), [o], [l, r])
+
+    def iota(o, pat, base, cm):
+        if SCRATCH[o[1]][2] == I4:
+            do("G", lambda: g.iota(o[0], pat, base, cm), [o], [])
+        else:
+            do("G", lambda: g.iota(o[0], pat, base, cm, allow_small_or_imprecise_dtypes=True), [o], [])
+
+    def keep(o, i, pat, cmp, fill, base, cm):
+        do("G", lambda: g.affine_select(o[0], i[0], pat, cmp, fill, base, cm), [o], [i])
+
+    def load(q, o, src, sem):
+        Q[q].dma_start(o[0], src).then_inc(T.sem[sem], 16)
+        note(q, sem, 16, [], [o])
+
+    def store(q, dst, i, sem):
+        need(q, [i], [])
+        Q[q].dma_start(dst, i[0]).then_inc(T.sem[sem], 16)
+
+    def engs(src, dsts):
+        e = [x for x in topo.engines(src, dsts[0]) if all(x in topo.engines(src, d) for d in dsts)]
+        n = 1
+        while 2 * n <= min(len(e), 8):
+            n *= 2
+        return e[:n]
+
+    def send(i, dsts, out, sem):
+        need("G", [i], [])
+        e = engs(core, dsts)
+        m = 0
+        for x in e:
+            m |= 1 << x
+        ids = []
+        for d in dsts:
+            rid, pid = topo.addr(d, core)
+            ids.append(DstId(rid=rid, pnc=pid))
+        g.remote_dma_fused([RemoteDMATransfer(dst_ids=ids, dma_engine_mask=m, remote_sem=T.sem[sem], srcs=[i[0]], dsts=[out for d in dsts])],
+                           local_sem=T.sem.loc)
+        sent[0] += len(e)
+
+    def land(o, sem, src, dsts):
+        note("R", sem, len(engs(src, dsts)), [], [o])
+
+    nxt = T.cores[(rank + STEP) % NG]
+    prv = T.cores[(rank - STEP) % NG]
+
+    def rest(j):
+        return [c for c in T.cores if c != T.cores[j]]
+
+    load("Y", A("P0R"), T.p0[:], "lp0")
+    load("S", A("X0R"), T.x0[:], "lx0")
+    for j in range(4):
+        load("Y" if j % 2 == 0 else "S", A("TXR", 512 * j, 512 * j + 512), T.tx[:, 512 * j:512 * j + 512], "ltx%d" % j)
+    for j in range(2):
+        load("Y", A("PU", 1024 * j, 1024 * j + 1024), T.pu[:, 1024 * j:1024 * j + 1024], "lpu%d" % j)
+
+    def col(j):
+        return A("PF", j, j + 1)
+
+    CK = [[0, 16], [1, 16]]
+    iota(A("PI", 0, 1), [[0, 1]], 0, 1)
+    iota(A("IF"), [[1, 144]], 0, 0)
+    iota(A("ONB"), [[0, 128]], 1, 0)
+    keep(A("ID"), A("ONB"), [[-1, 128]], OP.is_equal, 0.0, 0, 1)
+    act(A("NID"), A("ID"), scale=-1.0)
+    iota(A("KREV"), [[0, 16], [-1, 16]], 15, 0)
+    keep(A("KRV0"), A("KREV", 0, 128), [[0, 8], [1, 16]], OP.is_gt, -BIG, 0, 0)
+    iota(A("ONF"), [[0, 256]], 1, 0)
+    keep(A("RES1"), A("ONF"), CK, OP.is_equal, 0.0, 0, 0)
+    iota(A("NEGC"), [[0, 128]], -262144, 0)
+    keep(A("NEGM"), A("NEGC"), [[0, 8], [-1, 16]], OP.is_ge, 0.0, 14, 0)
+    keep(A("RES"), A("ONF"), CK, OP.is_gt, 0.0, 0, 0)
+    for r in range(NR):
+        iota(A("PA0" if r == 0 else "PAS%d" % r, 0, 1), [[0, 1]], 1, 0)
+    iota(A("MU"), [[0, 8], [1, 16]], 0, 0)
+    iota(A("MG"), [[1, 8], [0, 16]], 0, 0)
+    iota(A("IV"), [[1, 128]], 0, 0)
+    iota(A("KFW"), [[0, 8], [1, 16]], 0, 0)
+    iota(A("BASE"), [[16, 16]], 2048, 0)
+    iota(A("BKA"), [[0, 256]], 0, 0)
+    iota(A("BKB"), [[0, 256]], 0, 0)
+    iota(A("BGC"), [[0, 16], [-1, 16]], 262144 + 15, 0)
+    keep(A("BIGK"), A("BGC"), CK, OP.is_gt, 0.0, 0, 0)
+    AND, SHR = OP.bitwise_and, OP.arith_shift_right
+    ts(A("PI", 1, 2), A("PI", 0, 1), 15, AND)
+    ts(A("PI", 2, 3), A("PI", 0, 1), 4, SHR)
+    ts(A("PI", 3, 4), A("PI", 0, 1), 4, SHR, 1, AND)
+    ts(A("PI", 4, 5), A("PI", 0, 1), 112, AND)
+    cp(A("PF", 0, 5), A("PI", 0, 5))
+    ts(A("PF", 6, 7), A("PF", 3, 4), -1000.0, OP.mult)
+    ts(A("PF", 7, 8), A("PF", 3, 4), 1000.0, OP.mult, -1000.0, OP.add)
+    tt(A("PF", 8, 9), A("PF", 6, 7), A("PF", 0, 1), OP.add)
+    tt(A("PF", 9, 10), A("PF", 7, 8), A("PF", 0, 1), OP.add)
+    ts(A("PF", 10, 11), A("PF", 4, 5), 15.0, OP.add)
+    for x in range(2):
+        for y in range(2):
+            j = 2 * x + y
+            ts(A("SW", 128 * j, 128 * j + 128), A("IF", 0, 128), float(16 * (y - x)), OP.subtract, col(8 + x), OP.is_equal)
+
+    def swap(dst, src):
+        for x in range(2):
+            for y in range(2):
+                j = 2 * x + y
+                mm(B(T[dst][:, x:16:2, :], dst, 0, 16), A("SW", 128 * j, 128 * j + 128), B(T[src][:, y:16:2, :], src, 0, 16), y == 0, y == 1)
+
+    def offs(o):
+        for h in range(4):
+            ts(A(o, 64 * h, 64 * h + 64), A("PFL", h, 256, 4), 2048.0, OP.mult)
+
+    def spread(yn, c0, c1, q):
+        f = cp if q == "V" else (lambda o, i: act(o, i, AF.Copy))
+        X, y = T.XQ, A(yn, 16 * c0, 16 * c1)
+        f(B(X[:, c0:c1, 0, :], "XQ", 4 * c0, 4 * c0 + 1), y)
+        f(B(X[:, c0:c1, 1, :], "XQ", 4 * c0 + 1, 4 * c0 + 2), y)
+        f(B(X[:, c0:c1, 2:4, :], "XQ", 4 * c0 + 2, 4 * c0 + 4), B(X[:, c0:c1, 0:2, :], "XQ", 4 * c0, 4 * c0 + 2))
+        f(A("XR", 64 * c0, 64 * c1), B(X[:, c0:c1, :, :], "XQ", 4 * c0, 4 * c0 + 4))
+
+    for h in range(2):
+        ts(A("Y0", 128 * h, 128 * h + 128), A("X0R", h, 256, 2), -1.0, OP.mult, 256.0, OP.add)
+    spread("Y0", 0, 8, "V")
+    spread("Y0", 8, 16, "S")
+    for h in range(2):
+        cp(A("A16", 128 * h, 128 * h + 128), A("P0R", h, 256, 2))
+    t32(A("C16"), A("A16"))
+    swap("sps", "C16")
+    SD = B(T.sps[:, 0:16, :], "sps", 0, 16)
+    ts(A("PFL"), SD, 2.0 ** -11, OP.mult)
+    offs("PO0")
+    ts(A("FS"), A("IF"), col(10), OP.is_equal, 32.0, OP.mult)
+
+    def pay0():
+        act(A("TA"), A("PFL"), bias=1.0)
+        act(A("TB"), A("PFL"), scale=2.0 ** -11)
+
+    def pay1(pa):
+        tt(A(pa, 1, 256), A("TA", 1, 256), A("TB", 0, 255), OP.add)
+
+    def pens(km):
+        tt(A("EQ"), A("PFL", 0, 128), A("PFL", 128, 256), OP.is_equal)
+        scan(A("PRE"), A("RES1", 0, 128), A("EQ"), OP.max, OP.min)
+        tt(A("PM"), A("PRE"), A("NEGM"), OP.mult)
+        tt(A(km), A("PM"), A("KRV0"), OP.add)
+
+    for j in range(4):
+        o, i = A("TX", 512 * j, 512 * j + 512), A("TXR", 512 * j, 512 * j + 512)
+        if j % 2 == 0:
+            ts(o, i, -1.0, OP.mult, 256.0, OP.add)
+        else:
+            act(o, i, scale=-1.0, bias=256.0)
+    WIN = A("TX", 0, 2048)
+
+    def tables():
+        ts(A("BDM"), A("MG"), col(2), OP.is_equal)
+        ts(A("T1", 0, 128), A("MU"), 1.0, OP.add)
+        tt(A("T1", 128, 256), A("T1", 0, 128), A("BDM"), OP.mult)
+        ts(A("IU"), A("T1", 128, 256), -1.0, OP.add)
+
+    def tables2():
+        ts(A("BD"), A("BDM"), -256.0, OP.mult)
+        ts(A("H16"), A("IF", 0, 16), col(1), OP.is_equal)
+        for u in range(16):
+            ts(A("REP", 128 * u, 128 * u + 128), A("BD"), A("H16", u, u + 1), OP.mult)
+        ts(A("O1"), A("BASE"), col(1), OP.add)
+        ts(A("BASE"), A("O1"), 2.0 ** -11, OP.mult)
+
+    def dist(off, ps, ex, hooks=()):
+        do("S", lambda: g.scalar.activation(T.TG[:], T.TX[:, 0:2048].indirect(T[off][:, 32:64]), AF.Copy, bias=0.0, scale=1.0),
+           [A("TG")], [WIN, A(off, 32, 64)])
+        mm(A("t3"), A("ID"), A("TG"), True, False)
+        mm(A("t3"), A("NID"), A("XR", 512, 1024), False, True)
+        for h in range(4):
+            lo, hi = 1024 * h, 1024 * h + 1024
+            m = hi if h else lo + 512
+            gat(A("DF", lo, m), WIN, A(off, lo // 16, m // 16), A("XR", 0, m - lo), OP.subtract)
+            if h < len(hooks):
+                hooks[h]()
+            out = A(ps, h, 256, 4)
+            st = (1, 2, 2, 4)[h]
+            n = 0
+            for b0 in range(st):
+                nm = "AD%d_%d" % (h, b0)
+                act(B(T.AD[:, lo + b0:m:st], nm, lo, m), B(T.DF[:, lo + b0:m:st], "DF", lo, m), AF.Abs)
+                if h == 0:
+                    act(B(T.AD[:, m:hi], nm, m, hi), A("t3"), AF.Abs)
+                for b in range(b0, 16, st):
+                    mm(out, A("FS", 15 - b, 143 - b), B(T.AD[:, lo + b:hi:16], nm, lo, hi), n == 0, n == 15)
+                    n += 1
+                    if n == (4 if h == 3 else 14):
+                        for c in (0, 128):
+                            mm(A(ps, c + h, c + 128, 4), A("ID"), A(ex, h, 128, 4), False, False)
+
+    def latch(key, pay, res, o0, o1):
+        scan(A("FM"), A(res), key, o0, o1)
+        tt(A("RR"), key, A("FM"), OP.is_equal)
+        tt(A("D1"), pay, A("RR"), OP.subtract)
+        scan(A("LT"), A("RR"), A("D1"), OP.max, OP.min)
+
+    LAST = A("LT", 15, 256, 16)
+    FML = A("FM", 15, 256, 16)
+    DPS, EPS = A("dps", 0, 256), A("eps", 0, 256)
+    PAE = A("kps", 128, 384)
+    PAP = A("t2", 0, 256)
+    BGP = A("eps", 256, 512)
+    MPS = A("dps", 256, 384)
+    OH = A("dps", 256, 512)
+    PX = A("t0", 0, 256)
+    for r in range(NR):
+        last = r == NR - 1
+        Y, PO, KM, PA, MK, MS = ["%s%d" % (n, r) for n in ("Y", "PO", "KM", "PA", "MK", "MS")]
+        if r:
+            for n, s in ((Y, "ry"), (PO, "rp"), (KM, "rk"), (PA, "ra")):
+                land(A(n), "%s_%d" % (s, r), prv, [core])
+        if r:
+            spread(Y, 0, 8, "V")
+            spread(Y, 8, 16, "S")
+        else:
+            pay0()
+        dist(PO, "dps", KM, (lambda: pens("KM0"), tables, lambda: pay1("PA0")) if r == 0 else ())
+        act(A("TX", 2048, 2304), A(Y), AF.Copy)
+        act(PAP, A(PA), AF.Copy)
+        if r == 0:
+            act(A("RESB"), A("RES1"), scale=1048576.0)
+            act(BGP, A("BIGK"), AF.Copy)
+        else:
+            act(A("THA"), A(KM), AF.Relu, scale=-1.0)
+            for h in range(2):
+                act(A("THB", 128 * h, 128 * h + 128), A("THA"), scale=-1.0, bias=65536.0)
+        latch(DPS, PAP, "RES", OP.mult, OP.max)
+        ts(A("PAYI"), LAST, 4194304.0, OP.mult)
+        ts(A("UVI", 0, 16), A("PAYI"), 18, SHR)
+        ts(A("UVI", 16, 32), A("PAYI"), 11, SHR, 127, AND)
+        cp(A("UVF"), A("UVI"))
+        for c in range(16):
+            lo, hi = 128 * c, 128 * c + 128
+            ts(A("OU", lo, hi), A("IU"), A("UVF", c, c + 1), OP.is_equal)
+            ts(A("OV", lo, hi), A("IV"), A("UVF", 16 + c, 17 + c), OP.is_equal)
+            mm(MPS, A("OU", lo, hi), A("OV", lo, hi), c == 0, c == 15)
+        ts(A(MS), MPS, 0.5, OP.is_ge)
+        send(A(MS), rest(rank), T[MK][:, 128 * rank:128 * rank + 128], "mk%d_%d" % (r, rank))
+        for j in range(NG):
+            if j != rank:
+                land(A(MK, 128 * j, 128 * j + 128), "mk%d_%d" % (r, j), T.cores[j], rest(j))
+        if r:
+            tt(A("T1"), DPS, A("THB"), OP.is_ge)
+            tt(A("D1"), A("T1"), BGP, OP.mult)
+            tt(DPS, DPS, A("D1"), OP.max)
+            latch(DPS, PAP, "RES", OP.mult, OP.max)
+            ts(A("PAYI"), LAST, 4194304.0, OP.mult)
+        ts(A("TEI"), A("PAYI"), 2047, AND)
+        cp(A("TEO"), A("TEI"))
+        gat(A("A16"), A("PU"), A("TEO"))
+        t32(A("C16"), A("A16"))
+        swap("sps", "C16")
+        cp(A("DKI"), FML)
+        ts(A("PKI"), A("PAYI"), 11, SHR)
+        ts(A("DKJ"), A("DKI"), 15, AND)
+        ts(A("PK"), A("PKI"), 2.0 ** -11, OP.mult)
+        ts(A("DKM"), FML, 16.0, OP.subtract, 65536.0, OP.min)
+        cp(A("BKA", 0, 256, 16), A("DKJ"))
+        if r == 0:
+            tables2()
+        else:
+            for h in range(4):
+                ts(A("PFL", h, 256, 4), A(PO, 64 * h, 64 * h + 64), 2.0 ** -11, OP.mult)
+        scan(OH, A("RES"), A("BKA"), OP.mult, OP.add)
+        def bank(q, lo, hi):
+            return A("t%d" % q, lo, hi)
+        order = (3, 0, 2, 1)
+        for q in order:
+            mm(bank(q, 0, 512), A("ID"), A("TX", 512 * q, 512 * q + 512), True, False)
+        mm(A("kps", 0, 128), A("ID"), A(MS), True, False)
+        js = [j for j in range(NG) if j != rank]
+        for j in js:
+            mm(A("kps", 0, 128), A("ID"), A(MK, 128 * j, 128 * j + 128), False, j == js[-1])
+        ts(A("CUT"), A("kps", 0, 128), 3.5, OP.is_ge)
+        for q in order:
+            for u in range(4):
+                v = 4 * q + u
+                mm(bank(q, 128 * u, 128 * u + 128), A("REP", 128 * v, 128 * v + 128), A("CUT"), False, u == 3)
+        for h in range(4):
+            cp(A("PDO", 64 * h, 64 * h + 64), B(T.sps[:, 0:16, h:16:4], "sps", 0, 16))
+        for n, q in enumerate(order):
+            o = A("TX", 512 * q, 512 * q + 512)
+            if n % 2 == 0:
+                ts(o, bank(q, 0, 512), 0.0, OP.max)
+                if n == 0:
+                    tt(OH, OH, A("KREV"), OP.is_equal)
+            else:
+                act(o, bank(q, 0, 512), AF.Relu)
+        dist("PDO", "eps", "KFW")
+        if r == 0:
+            cp(A("CAC"), A("CUT"))
+        else:
+            tt(A("CA2" if r == 1 else "CAC"), A("CAC" if r == 1 else "CA2"), A("CUT"), OP.max)
+        ts(PAE, SD, 2.0 ** -11, OP.mult, 1.0, OP.add)
+        tt(PX, OH, A("PFL"), OP.mult)
+        tt(A("PZ"), A("PFL"), PX, OP.subtract)
+        latch(EPS, PAE, "RESB", OP.add, OP.min)
+        tt(A("O1"), LAST, A("BASE"), OP.subtract)
+        tt(A("TK"), A("DKM"), FML, OP.is_ge)
+        tt(A("N1"), LAST, A("PK"), OP.subtract)
+        tt(A("O2"), A("O1"), A("TK"), OP.mult)
+        tt(A("N2"), A("N1"), A("TK"), OP.mult)
+        tt(A("OF"), A("O2"), A("BASE"), OP.add)
+        tt(A("BKB", 0, 256, 16), A("N2"), A("PK"), OP.add)
+        ts(A("OFO"), A("OF"), 2048.0, OP.mult)
+        gat(A("SU"), A("TX"), A("OFO"), A(Y), OP.add)
+        e = r + 1
+        YS = "YS%d" % e
+        act(A(YS), A("SU"), scale=0.5, bias=0.25)
+        if not last:
+            send(A(YS), [nxt], T["Y%d" % e][:], "ry_%d" % e)
+        NB, NV = A("T1"), A("t0", 256, 512)
+        scan(NB, A("RES"), A("BKB"), OP.mult, OP.add)
+        tt(NV, OH, NB, OP.mult)
+        if not last:
+            tt(A("PFL"), A("PZ"), NV, OP.add)
+            offs("POS%d" % e)
+            send(A("POS%d" % e), [nxt], T["PO%d" % e][:], "rp_%d" % e)
+            pay0()
+            pens("KMS%d" % e)
+            pay1("PAS%d" % e)
+            send(A("KMS%d" % e), [nxt], T["KM%d" % e][:], "rk_%d" % e)
+            send(A("PAS%d" % e), [nxt], T["PA%d" % e][:], "ra_%d" % e)
+        else:
+            tt(A("PNH"), A("PZ"), NV, OP.add)
+            swap("sps", "PNH")
+            for h in range(2):
+                act(A("YXB", h, 256, 2), A(YS, 128 * h, 128 * h + 128), scale=-1.0, bias=256.0)
+            store("Y", T.yx[:], A("YXB"), "oyx")
+            store("Y", T.yc[:], A("CAC"), "oyc")
+            t32(A("YPA"), SD)
+            ts(A("YPB", 0, 256, 2), A("YPA", 0, 128), 2048.0, OP.mult)
+            act(A("YPB", 1, 256, 2), A("YPA", 128, 256), scale=2048.0)
+            store("Y", T.yp[:], A("YPB"), "oyp")
+
+    for s in ["oyp", "oyx", "oyc"] + LOADS:
+        g.sync.wait_ge(T.sem[s], 16)
+    g.wait_ge(T.sem.loc, sent[0])
+    for q in ("V", "S", "P", "G"):
+        g.wait_ge(T.sem[SEM[q]], cnt[q])

@@ -1,47 +1,98 @@
+import numpy as np
 from concourse.bass import DstId, RemoteDMATransfer
-from concourse.mybir import dt, AluOpType as OP, ActivationFunctionType as AF
+from concourse.mybir import AluOpType as OP, ActivationFunctionType as AF
 
 NR = 3
 STEP = 5
 NG = 8
-BIG = 262144.0
+W = 2048
+CUTKEY = 65536.0
+M2, M32 = 1.5 * 2 ** 24, 1.5 * 2 ** 18
+OFF = 991.5 / 2048
+XO = 1536.0
 
 F4, BF, HF, I4, U2 = "float32", "bfloat16", "float16", "int32", "uint16"
 SCRATCH = {}
 for _n, _w, _d in (
-        ("TXR", 2048, BF), ("TX", 2304, BF), ("PU", 2048, I4), ("P0R", 256, I4), ("X0R", 256, BF),
-        ("XR", 1024, BF), ("DF", 4096, BF), ("AD", 4096, BF), ("TG", 512, BF), ("OU", 2048, BF), ("OV", 2048, BF),
-        ("PI", 8, I4), ("PF", 12, F4), ("IF", 144, F4), ("MU", 128, F4), ("MG", 128, F4), ("FS", 144, BF), ("ID", 128, BF), ("NID", 128, BF),
-        ("SW", 512, HF), ("ONB", 128, BF), ("ONF", 256, F4), ("NEGC", 128, F4), ("BGC", 256, F4), ("REP", 2048, BF), ("BD", 128, BF),
-        ("H16", 16, F4), ("IU", 128, BF), ("IV", 128, BF), ("BDM", 128, F4), ("KREV", 256, F4), ("KFW", 128, BF), ("KRV0", 128, F4),
-        ("NEGM", 128, F4), ("RES", 256, F4), ("RES1", 256, F4), ("RESB", 256, F4), ("BIGK", 256, F4), ("BASE", 16, F4), ("BKA", 256, F4), ("BKB", 256, F4),
-        ("A16", 256, HF), ("PFL", 256, F4), ("FM", 256, F4), ("RR", 256, F4), ("D1", 256, F4), ("LT", 256, F4), ("PAYI", 16, I4), ("UVI", 32, I4),
-        ("UVF", 32, F4), ("TEI", 16, I4), ("TEO", 16, U2), ("PKI", 16, I4), ("PK", 16, F4), ("DKM", 16, F4), ("DKI", 16, I4), ("DKJ", 16, I4),
-        ("PZ", 256, F4), ("THA", 128, F4), ("THB", 256, F4), ("T1", 256, F4), ("PDO", 256, U2), ("CUT", 128, BF),
-        ("CAC", 128, F4), ("CA2", 128, F4), ("TK", 16, F4), ("O1", 16, F4), ("O2", 16, F4), ("OF", 16, F4), ("OFO", 16, U2),
-        ("N1", 16, F4), ("N2", 16, F4), ("SU", 256, F4), ("EQ", 128, F4), ("PRE", 128, F4), ("PM", 128, F4), ("TA", 256, F4), ("TB", 256, F4),
-        ("YPA", 256, F4), ("YPB", 256, F4), ("YXB", 256, BF)):
+        ("PI", 8, I4), ("PF", 12, F4), ("IF", 144, F4), ("FS", 144, BF), ("FN", 144, BF), ("ID", 128, BF), ("NID", 128, BF), ("ID64", 128, BF), ("IDH", 128, HF),
+        ("SW", 512, HF), ("CF", 256, HF), ("KA", 128, BF), ("KG", 256, BF), ("EX1", 128, BF), ("EX2", 128, BF), ("RES", 256, BF), ("RESB", 128, BF),
+        ("IU", 128, BF), ("IV", 64, BF), ("RB", 128, BF), ("C256", 128, BF), ("REP", 4096, BF), ("B0", 8, F4), ("BASE", 8, F4)):
     SCRATCH[_n] = ("sbuf", [128, _w], _d)
-SCRATCH["XQ"] = ("sbuf", [128, 16, 4, 16], BF)
-for _n in ("C16", "PNH"):
-    SCRATCH[_n] = ("sbuf", [128, 16, 16], HF)
-SCRATCH["sps"] = ("psum", [128, 32, 16], F4)
-for _n in ("dps", "eps", "kps", "t0", "t1", "t2", "t3"):
-    SCRATCH[_n] = ("psum", [128, 512], F4)
-for _r in range(NR):
-    SCRATCH["Y%d" % _r] = ("sbuf", [128, 256], BF)
-    SCRATCH["YS%d" % (_r + 1)] = ("sbuf", [128, 256], BF)
-    for _s in ("", "S") if _r else ("",):
-        SCRATCH["PO%s%d" % (_s, _r)] = ("sbuf", [128, 256], U2)
-        SCRATCH["KM%s%d" % (_s, _r)] = ("sbuf", [128, 128], BF)
-        SCRATCH["PA%s%d" % (_s, _r)] = ("sbuf", [128, 256], F4)
-    SCRATCH["MK%d" % _r] = ("sbuf", [128, 1024], BF)
-    SCRATCH["MS%d" % _r] = ("sbuf", [128, 128], BF)
+for _s in range(2):
+    for _n, _w, _d in (
+            ("TX", W + 512, BF), ("PU", W, I4), ("P0R", 128, I4), ("X0R", 128, BF), ("RL", 256 * NR, HF), ("RS", 256 * NR, HF),
+            ("PO", 128, U2), ("PD", 128, U2), ("RQ", 128, BF), ("NE", 64, BF), ("FM", 128, F4), ("NR", 128, BF),
+            ("LL", 256, F4), ("GL", 256, F4), ("SG", 128, BF), ("SM", 128, F4), ("TEO", 8, U2), ("OFO", 8, U2), ("BKA", 128, BF), ("BKB", 128, HF),
+            ("OH", 128, BF), ("MK", 64 * NG * NR, BF), ("CT", 64 * NR, BF), ("YC", 64, F4), ("YP", 128, F4), ("YX", 128, BF),
+            ("DF", 2048, BF), ("TG", 2048, BF), ("OU", 1024, BF), ("OV", 512, BF), ("A16", 128, HF), ("D1", 128, F4), ("F3", 128, F4),
+            ("L3", 128, F4), ("OS", 128, BF), ("SU", 128, HF), ("YPA", 128, F4)):
+        SCRATCH["%s%d" % (_n, _s)] = ("sbuf", [128, _w], _d)
+    SCRATCH["XQ%d" % _s] = ("sbuf", [128, 8, 4, 16], BF)
+    SCRATCH["AD%d" % _s] = ("sbuf", [128, 8, 16, 16], BF)
+    for _n in ("PN", "C16"):
+        SCRATCH["%s%d" % (_n, _s)] = ("sbuf", [128, 8, 16], HF)
+    SCRATCH["sp%d" % _s] = ("psum", [128, 32, 16], F4)
+    for _n in ("k", "ta", "tb"):
+        SCRATCH["%s%d" % (_n, _s)] = ("psum", [128, 512], F4)
 PSUM = [n for n in SCRATCH if SCRATCH[n][0] == "psum"]
 
-LOADS = ["lp0", "lx0", "ltx0", "ltx1", "ltx2", "ltx3", "lpu0", "lpu1"]
-SEMAPHORES = (["qv", "qs", "qp", "qg", "loc", "oyp", "oyx", "oyc"] + LOADS + ["mk%d_%d" % (r, j) for r in range(NR) for j in range(NG)]
-              + ["%s_%d" % (n, r) for r in range(1, NR) for n in ("ry", "rp", "rk", "ra")])
+LOADS = ["l%s%d" % (n, s) for s in range(2) for n in ("p0", "x0", "tx", "pu")]
+STORES = ["o%s%d" % (n, s) for s in range(2) for n in ("yp", "yx", "yc")]
+SEMAPHORES = (["qv", "qs", "qp", "qg", "loc"] + LOADS + STORES + ["mk%d_%d" % (s, r) for s in range(2) for r in range(NR)]
+              + ["rg%d_%d" % (s, r) for s in range(2) for r in range(1, NR)])
+
+CHAINS, PUPILS, QUARTERS, SPREAD, PARITY = "SSRR", "SSRR", "SVSS", "S", (0, 1)
+CYCLE, PECYCLE, GATHER, WAKE = 1.04e-3, 0.52e-3, 1.56, 0.07
+TABLES, RING, FIRST = 5.5, 4.2, 2.8
+ARRIVE = {"lp00": 2.2, "lx00": 2.5, "ltx0": 4.8, "lp01": 5.3, "lx01": 5.7, "ltx1": 8.8, "lpu0": 14.0, "lpu1": 20.0}
+LEAD = 8.0
+ORDER, MASKS = [], {}
+
+
+def place(ops, order, deps, at):
+    start, busy = {}, {}
+    for i in order:
+        o = ops[i]
+        t = max([at[i]] + [start[j] + ops[j]["dur"] + lat for j, lat in deps[i].items() if j in start])
+        if o["dur"]:
+            line = busy.setdefault(o["q"], [])
+            n = 0
+            while n < len(line) and line[n][0] < t + o["dur"]:
+                t = max(t, line[n][1])
+                n += 1
+            line.insert(n, (t, t + o["dur"]))
+        start[i] = t
+    return start
+
+
+def improve(ops, order, fw, bw, passes):
+    for it in range(passes):
+        st = place(ops, order, fw, [o["at"] for o in ops])
+        back = place(ops, sorted(order, key=lambda i: (-st[i] - ops[i]["dur"], -i)), bw, [0.0] * len(ops))
+        order = sorted(order, key=lambda i: (-back[i] - ops[i]["dur"], i))
+    return st, back
+
+
+def issue_order(ops):
+    n = len(ops)
+    fw, bw = [o["deps"] for o in ops], [{} for o in ops]
+    way = [0.0] * n
+    for i in range(n - 1, -1, -1):
+        way[i] += ops[i]["dur"]
+        for j, lat in fw[i].items():
+            bw[j][i] = lat
+            way[j] = max(way[j], way[i] + lat)
+    m = sum(o["set"] for o in ops)
+    one = sorted(range(n - m), key=lambda i: (-way[i], i))
+    st, back = improve(ops, one, fw, bw, 2)
+    late = {i: -back[i] - ops[i]["dur"] for i in one}
+    for i in range(n - m, n):
+        late[i] = late[i - m] + LEAD
+    for i in range(n - 1, -1, -1):
+        for j in fw[i]:
+            late[j] = min(late[j], late[i])
+    st, back = improve(ops, sorted(range(n), key=lambda i: (late[i], i)), fw, bw, 2)
+    return sorted(range(n), key=lambda i: (st[i], i))
 
 
 def rank_program(g, core, T, topo):
@@ -50,417 +101,461 @@ def rank_program(g, core, T, topo):
         return
     Q = {"V": g.vector, "S": g.scalar, "P": g.tensor, "G": g, "Y": g.sync}
     SEM = {"V": "qv", "S": "qs", "P": "qp", "G": "qg"}
-    cnt = {"V": 0, "S": 0, "P": 0, "G": 0}
-    known = {q: {} for q in Q}
-    acc = {}
+    ALL = slice(None)
+    masks = MASKS
     sent = [0]
+
+    def N(n, *ix):
+        key = (n, repr(ix))
+        if key not in masks:
+            m = np.zeros(SCRATCH[n][1][1:], np.uint8)
+            m[ix] = 1
+            masks[key] = (int.from_bytes(np.packbits(m.reshape(-1), bitorder="little").tobytes(), "little"), int(m.sum()))
+        return (T[n][(ALL,) + ix], n) + masks[key]
 
     def A(n, lo=0, hi=None, st=1):
         hi = SCRATCH[n][1][1] if hi is None else hi
-        return (T[n][:, lo:hi] if st == 1 else T[n][:, lo:hi:st], n, lo, hi)
+        return N(n, slice(lo, hi) if st == 1 else slice(lo, hi, st))
 
-    def B(ap, n, lo, hi):
-        return (ap, n, lo, hi)
+    def clash(q, isw, n, m, e):
+        return (n in PSUM and e[2] != q) or ((isw or e[1]) and m & e[0])
 
-    def need(q, ins, outs):
-        w = {}
-        for isw, ops in ((False, ins), (True, outs)):
-            for (_, n, lo, hi) in ops:
-                for (l2, h2, w2, q2, s2, v2) in acc.get(n, ()):
-                    ps = n in PSUM
-                    if ps and q2 == q and q == "P":
-                        continue
-                    hit = ps and q2 != q
-                    hit = hit or ((isw or w2) and lo < h2 and l2 < hi)
-                    if hit and known[q].get(s2, 0) < v2:
-                        w[s2] = max(w.get(s2, 0), v2)
-        for s in sorted(w):
-            Q[q].wait_ge(T.sem[s], w[s])
-            known[q][s] = w[s]
+    ops, seen, now = [], {}, [0]
 
-    def note(q, s, v, ins, outs):
-        for (_, n, lo, hi) in outs:
-            acc[n] = [e for e in acc.get(n, []) if (e[3] == q or n not in PSUM) and not (lo <= e[0] and e[1] <= hi)]
-            acc[n].append((lo, hi, True, q, s, v))
-        for (_, n, lo, hi) in ins:
-            acc.setdefault(n, []).append((lo, hi, False, q, s, v))
+    def put(q, f, outs, ins, dur, sem=None, at=0.0, after=None):
+        deps = dict([after]) if after else {}
+        for isw, xs in ((False, ins), (True, outs)):
+            for (_, n, m, _c) in xs:
+                for e in seen.get(n, ()):
+                    if q == e[2] == "P" and n in PSUM:
+                        deps[e[3]] = 0.0
+                    elif clash(q, isw, n, m, e):
+                        deps[e[3]] = WAKE
+        for (_, n, m, _c) in outs:
+            seen[n] = [e for e in seen.get(n, []) if (e[2] == q or n not in PSUM) and e[0] & ~m] + [(m, True, q, len(ops))]
+        for (_, n, m, _c) in ins:
+            seen.setdefault(n, []).append((m, False, q, len(ops)))
+        ops.append({"q": q, "f": f, "outs": outs, "ins": ins, "dur": dur, "sem": sem, "at": at, "deps": deps, "set": now[0]})
+        return len(ops) - 1
 
-    def do(q, f, outs, ins):
-        need(q, ins, outs)
-        f().then_inc(T.sem[SEM[q]], 1)
-        cnt[q] += 1
-        note(q, SEM[q], cnt[q], ins, outs)
+    def issue():
+        cnt = {q: 0 for q in SEM}
+        known = {q: {} for q in Q}
+        past, acc = {}, {}
+        if not ORDER:
+            ORDER.extend(issue_order(ops))
+        for o in [ops[i] for i in ORDER]:
+            q, w = o["q"], {}
+            if q in Q:
+                for isw, xs in ((False, o["ins"]), (True, o["outs"] if o["sem"] is None else [])):
+                    for (_, n, m, _c) in xs:
+                        for e in acc.get(n, ()):
+                            if not (q == e[2] == "P" and n in PSUM) and clash(q, isw, n, m, e) and known[q].get(e[3], 0) < e[4]:
+                                w[e[3]] = max(w.get(e[3], 0), e[4])
+                for s in sorted(w, key=lambda s: -len(past.get((s, w[s]), ()))):
+                    if known[q].get(s, 0) < w[s]:
+                        Q[q].wait_ge(T.sem[s], w[s])
+                        known[q][s] = w[s]
+                        for s2, v2 in past.get((s, w[s]), {}).items():
+                            known[q][s2] = max(known[q].get(s2, 0), v2)
+            if o["sem"] is None:
+                o["f"]().then_inc(T.sem[SEM[q]], 1)
+                cnt[q] += 1
+                s, v = SEM[q], cnt[q]
+                past[(s, v)] = dict(known[q])
+            else:
+                if o["f"]:
+                    o["f"]()
+                s, v = o["sem"]
+                if not v:
+                    continue
+            for (_, n, m, _c) in o["outs"]:
+                acc[n] = [e for e in acc.get(n, []) if (e[2] == q or n not in PSUM) and e[0] & ~m] + [(m, True, q, s, v)]
+            for (_, n, m, _c) in o["ins"]:
+                acc[n] = [e for e in acc.get(n, []) if not (e[0] == m and not e[1] and e[3] == s)] + [(m, False, q, s, v)]
+        return cnt
+
+    def vec(f, o, ins, k=None, extra=()):
+        if k is None:
+            k = 0.5 if all(SCRATCH[x[1]][2] in (BF, HF, U2) for x in [o] + ins) else 1
+        put("V", f, [o], ins + list(extra), 0.03 + max(64, k * o[3]) * CYCLE)
 
     def cp(o, i):
-        do("V", lambda: g.vector.tensor_copy(o[0], i[0]), [o], [i])
+        vec(lambda: g.vector.tensor_copy(o[0], i[0]), o, [i])
+
+    def fill(o, v):
+        vec(lambda: g.vector.memset(o[0], v), o, [])
 
     def tt(o, a, b, op):
-        do("V", lambda: g.vector.tensor_tensor(o[0], a[0], b[0], op), [o], [a, b])
+        vec(lambda: g.vector.tensor_tensor(o[0], a[0], b[0], op), o, [a, b], 1 if a[1] in PSUM or b[1] in PSUM else 2)
 
     def ts(o, a, s1, op0, s2=None, op1=None):
         extra = [s for s in (s1, s2) if isinstance(s, tuple)]
         v1 = s1[0] if isinstance(s1, tuple) else s1
         v2 = s2[0] if isinstance(s2, tuple) else s2
         if op1 is None:
-            do("V", lambda: g.vector.tensor_scalar(o[0], a[0], v1, None, op0), [o], [a] + extra)
+            vec(lambda: g.vector.tensor_scalar(o[0], a[0], v1, None, op0), o, [a], None, extra)
         else:
-            do("V", lambda: g.vector.tensor_scalar(o[0], a[0], v1, v2, op0, op1), [o], [a] + extra)
+            vec(lambda: g.vector.tensor_scalar(o[0], a[0], v1, v2, op0, op1), o, [a], None, extra)
 
     def scan(o, d0, d1, op0, op1):
-        do("V", lambda: g.vector.tensor_tensor_scan(o[0], d0[0], d1[0], 0.0, op0, op1), [o], [d0, d1])
+        vec(lambda: g.vector.tensor_tensor_scan(o[0], d0[0], d1[0], 0.0, op0, op1), o, [d0, d1])
 
     def t32(o, i):
-        do("V", lambda: g.vector.transpose(o[0], i[0]), [o], [i])
+        vec(lambda: g.vector.transpose(o[0], i[0]), o, [i])
 
-    def gat(o, win, off, in1=None, op=None):
+    def gat(o, win, off, in1, op):
         ap = win[0].indirect(off[0])
-        if in1 is None:
-            do("V", lambda: g.vector.tensor_copy(o[0], ap), [o], [win, off])
+        if isinstance(in1, tuple):
+            vec(lambda: g.vector.tensor_tensor(o[0], ap, in1[0], op), o, [win, off, in1], GATHER)
         else:
-            do("V", lambda: g.vector.tensor_tensor(o[0], ap, in1[0], op), [o], [win, off, in1])
+            vec(lambda: g.vector.tensor_scalar(o[0], ap, in1, None, op), o, [win, off], GATHER)
 
-    def act(o, i, func=AF.Identity, scale=1.0, bias=0.0):
-        do("S", lambda: g.scalar.activation(o[0], i[0], func, bias=bias, scale=scale), [o], [i])
+    def act(o, i, func=AF.Identity, scale=1.0, bias=0.0, off=None):
+        ap = i[0].indirect(off[0]) if off else i[0]
+        put("S", lambda: g.scalar.activation(o[0], ap, func, bias=bias, scale=scale), [o], [i, off] if off else [i],
+            0.06 + max(64, o[3] * (GATHER if off else 1)) * CYCLE)
 
-    def mm(o, l, r, start, stop):
-        do("P", lambda: g.tensor.matmul(o[0], l[0], r[0], start, stop), [o], [l, r])
+    def mm(o, l, r, start, stop, after=None):
+        return put("P", lambda: g.tensor.matmul(o[0], l[0], r[0], start, stop), [o], [l, r], max(64, o[3]) * PECYCLE, after=after)
 
     def iota(o, pat, base, cm):
         if SCRATCH[o[1]][2] == I4:
-            do("G", lambda: g.iota(o[0], pat, base, cm), [o], [])
+            put("G", lambda: g.iota(o[0], pat, base, cm), [o], [], 0.13)
         else:
-            do("G", lambda: g.iota(o[0], pat, base, cm, allow_small_or_imprecise_dtypes=True), [o], [])
+            put("G", lambda: g.iota(o[0], pat, base, cm, allow_small_or_imprecise_dtypes=True), [o], [], 0.13 + 2 * o[3] * CYCLE)
 
-    def keep(o, i, pat, cmp, fill, base, cm):
-        do("G", lambda: g.affine_select(o[0], i[0], pat, cmp, fill, base, cm), [o], [i])
+    def keep(o, i, pat, cmp, fillv, base, cm):
+        put("G", lambda: g.affine_select(o[0], i[0], pat, cmp, fillv, base, cm), [o], [i], 0.17 + 2 * o[3] * CYCLE)
 
-    def load(q, o, src, sem):
-        Q[q].dma_start(o[0], src).then_inc(T.sem[sem], 16)
-        note(q, sem, 16, [], [o])
+    def load(qs, n, s, src, w, sem, after=None):
+        for d in range(2):
+            if after:
+                Q[qs[d]].wait_ge(T.sem[after], 32)
+            rows = src[64 * s:64 * s + 64, :] if w == W else src[64 * s:64 * s + 64, w * d:w * d + w]
+            Q[qs[d]].dma_start(T[n][64 * d:64 * d + 64, 0:w], rows).then_inc(T.sem[sem], 16)
+        put("R", None, [A(n, 0, w)], [], 0.0, (sem, 32), ARRIVE[sem])
 
-    def store(q, dst, i, sem):
-        need(q, [i], [])
-        Q[q].dma_start(dst, i[0]).then_inc(T.sem[sem], 16)
+    def store(qs, dst, n, s, sem):
+        for d in range(2):
+            put(qs[d], lambda d=d: Q[qs[d]].dma_start(dst[64 * s:64 * s + 64, 128 * d:128 * d + 128],
+                                                      T[n][64 * d:64 * d + 64, :]).then_inc(T.sem[sem], 16), [], [A(n)], 0.05, (sem, 0))
 
-    def engs(src, dsts):
-        e = [x for x in topo.engines(src, dsts[0]) if all(x in topo.engines(src, d) for d in dsts)]
+    def pow2(e):
         n = 1
-        while 2 * n <= min(len(e), 8):
+        while 2 * n <= len(e):
             n *= 2
         return e[:n]
 
-    def send(i, dsts, out, sem):
-        need("G", [i], [])
-        e = engs(core, dsts)
-        m = 0
-        for x in e:
-            m |= 1 << x
-        ids = []
-        for d in dsts:
-            rid, pid = topo.addr(d, core)
-            ids.append(DstId(rid=rid, pnc=pid))
-        g.remote_dma_fused([RemoteDMATransfer(dst_ids=ids, dma_engine_mask=m, remote_sem=T.sem[sem], srcs=[i[0]], dsts=[out for d in dsts])],
-                           local_sem=T.sem.loc)
-        sent[0] += len(e)
+    def common(src, dsts):
+        return [x for x in topo.engines(src, dsts[0]) if all(x in topo.engines(src, d) for d in dsts)]
 
-    def land(o, sem, src, dsts):
-        note("R", sem, len(engs(src, dsts)), [], [o])
+    def spread_plan(src):
+        near = [c for c in T.cores if c != src and c in topo.cores_of(src)]
+        far = [c for c in T.cores if c not in topo.cores_of(src)]
+        ef = pow2(common(src, far))
+        return [(far, ef), (near, pow2([x for x in common(src, near) if x not in ef]))]
+
+    def send(parts, sem, lands, count, lat):
+        trs = []
+        for i, out, dsts, e in parts:
+            ids = [DstId(rid=topo.addr(d, core)[0], pnc=topo.addr(d, core)[1]) for d in dsts]
+            trs.append(RemoteDMATransfer(dst_ids=ids, dma_engine_mask=sum(1 << x for x in e), remote_sem=T.sem[sem],
+                                         srcs=[i[0]], dsts=[out[0] for d in dsts]))
+        lat += 0.0 if sent[0] else FIRST
+        sent[0] += sum(len(p[3]) for p in parts)
+        j = put("G", lambda: g.remote_dma_fused(trs, local_sem=T.sem.loc), [], [p[0] for p in parts], 0.9, (sem, 0))
+        put("R", None, lands, [], 0.0, (sem, count), 0.0, (j, lat - 0.9))
 
     nxt = T.cores[(rank + STEP) % NG]
     prv = T.cores[(rank - STEP) % NG]
 
-    def rest(j):
-        return [c for c in T.cores if c != T.cores[j]]
-
-    load("Y", A("P0R"), T.p0[:], "lp0")
-    load("S", A("X0R"), T.x0[:], "lx0")
-    for j in range(4):
-        load("Y" if j % 2 == 0 else "S", A("TXR", 512 * j, 512 * j + 512), T.tx[:, 512 * j:512 * j + 512], "ltx%d" % j)
-    for j in range(2):
-        load("Y", A("PU", 1024 * j, 1024 * j + 1024), T.pu[:, 1024 * j:1024 * j + 1024], "lpu%d" % j)
+    load("YS", "P0R0", 0, T.p0, 128, "lp00")
+    load("YS", "X0R0", 0, T.x0, 128, "lx00")
+    load("YS", "TX0", 0, T.tx, W, "ltx0")
+    load("YY", "P0R1", 1, T.p0, 128, "lp01")
+    load("YY", "X0R1", 1, T.x0, 128, "lx01")
+    load("YY", "TX1", 1, T.tx, W, "ltx1", "ltx0")
+    load("YY", "PU0", 0, T.pu, W, "lpu0", "ltx1")
+    load("YY", "PU1", 1, T.pu, W, "lpu1", "lpu0")
 
     def col(j):
         return A("PF", j, j + 1)
 
-    CK = [[0, 16], [1, 16]]
     iota(A("PI", 0, 1), [[0, 1]], 0, 1)
     iota(A("IF"), [[1, 144]], 0, 0)
-    iota(A("ONB"), [[0, 128]], 1, 0)
-    keep(A("ID"), A("ONB"), [[-1, 128]], OP.is_equal, 0.0, 0, 1)
-    act(A("NID"), A("ID"), scale=-1.0)
-    iota(A("KREV"), [[0, 16], [-1, 16]], 15, 0)
-    keep(A("KRV0"), A("KREV", 0, 128), [[0, 8], [1, 16]], OP.is_gt, -BIG, 0, 0)
-    iota(A("ONF"), [[0, 256]], 1, 0)
-    keep(A("RES1"), A("ONF"), CK, OP.is_equal, 0.0, 0, 0)
-    iota(A("NEGC"), [[0, 128]], -262144, 0)
-    keep(A("NEGM"), A("NEGC"), [[0, 8], [-1, 16]], OP.is_ge, 0.0, 14, 0)
-    keep(A("RES"), A("ONF"), CK, OP.is_gt, 0.0, 0, 0)
-    for r in range(NR):
-        iota(A("PA0" if r == 0 else "PAS%d" % r, 0, 1), [[0, 1]], 1, 0)
-    iota(A("MU"), [[0, 8], [1, 16]], 0, 0)
-    iota(A("MG"), [[1, 8], [0, 16]], 0, 0)
-    iota(A("IV"), [[1, 128]], 0, 0)
-    iota(A("KFW"), [[0, 8], [1, 16]], 0, 0)
-    iota(A("BASE"), [[16, 16]], 2048, 0)
-    iota(A("BKA"), [[0, 256]], 0, 0)
-    iota(A("BKB"), [[0, 256]], 0, 0)
-    iota(A("BGC"), [[0, 16], [-1, 16]], 262144 + 15, 0)
-    keep(A("BIGK"), A("BGC"), CK, OP.is_gt, 0.0, 0, 0)
+    iota(A("KA"), [[0, 8], [-2, 16]], 32, 0)
+    iota(A("EX1"), [[0, 8], [-1, 16]], 15, 0)
+    iota(A("EX2"), [[0, 8], [1, 16]], 17, 0)
+    iota(A("B0"), [[64, 8]], W, 0)
+    RPAT = [[0, 2], [-32, 4], [0, 16]]
+    iota(A("RB"), RPAT, 0, 1)
+    for h in range(2):
+        iota(A("KG", 128 * h, 128 * h + 128), [[0, 8], [-2, 16]], 2 * h - 32, 0)
     AND, SHR = OP.bitwise_and, OP.arith_shift_right
     ts(A("PI", 1, 2), A("PI", 0, 1), 15, AND)
-    ts(A("PI", 2, 3), A("PI", 0, 1), 4, SHR)
+    ts(A("PI", 2, 3), A("PI", 0, 1), 48, AND)
     ts(A("PI", 3, 4), A("PI", 0, 1), 4, SHR, 1, AND)
     ts(A("PI", 4, 5), A("PI", 0, 1), 112, AND)
+    fill(A("RES"), 1.0)
+    fill(A("RESB"), 0.0)
+    fill(A("C256"), 256.0)
     cp(A("PF", 0, 5), A("PI", 0, 5))
-    ts(A("PF", 6, 7), A("PF", 3, 4), -1000.0, OP.mult)
-    ts(A("PF", 7, 8), A("PF", 3, 4), 1000.0, OP.mult, -1000.0, OP.add)
-    tt(A("PF", 8, 9), A("PF", 6, 7), A("PF", 0, 1), OP.add)
-    tt(A("PF", 9, 10), A("PF", 7, 8), A("PF", 0, 1), OP.add)
-    ts(A("PF", 10, 11), A("PF", 4, 5), 15.0, OP.add)
+    fill(A("RES", 0, 256, 16), 0.0)
+    fill(A("RESB", 0, 128, 16), 2.0 ** 22)
+    ts(col(6), col(3), -1000.0, OP.mult, col(0), OP.add)
+    ts(col(8), col(3), 1000.0, OP.mult, -1000.0, OP.add)
+    ts(col(9), col(4), 15.0, OP.add)
+    ts(col(10), col(2), 2.0, OP.mult, 15.0, OP.add)
+    ts(col(7), col(8), col(0), OP.add)
+    ts(A("ID"), A("IF", 0, 128), col(0), OP.is_equal)
     for x in range(2):
         for y in range(2):
             j = 2 * x + y
-            ts(A("SW", 128 * j, 128 * j + 128), A("IF", 0, 128), float(16 * (y - x)), OP.subtract, col(8 + x), OP.is_equal)
-
-    def swap(dst, src):
-        for x in range(2):
-            for y in range(2):
-                j = 2 * x + y
-                mm(B(T[dst][:, x:16:2, :], dst, 0, 16), A("SW", 128 * j, 128 * j + 128), B(T[src][:, y:16:2, :], src, 0, 16), y == 0, y == 1)
-
-    def offs(o):
-        for h in range(4):
-            ts(A(o, 64 * h, 64 * h + 64), A("PFL", h, 256, 4), 2048.0, OP.mult)
-
-    def spread(yn, c0, c1, q):
-        f = cp if q == "V" else (lambda o, i: act(o, i, AF.Copy))
-        X, y = T.XQ, A(yn, 16 * c0, 16 * c1)
-        f(B(X[:, c0:c1, 0, :], "XQ", 4 * c0, 4 * c0 + 1), y)
-        f(B(X[:, c0:c1, 1, :], "XQ", 4 * c0 + 1, 4 * c0 + 2), y)
-        f(B(X[:, c0:c1, 2:4, :], "XQ", 4 * c0 + 2, 4 * c0 + 4), B(X[:, c0:c1, 0:2, :], "XQ", 4 * c0, 4 * c0 + 2))
-        f(A("XR", 64 * c0, 64 * c1), B(X[:, c0:c1, :, :], "XQ", 4 * c0, 4 * c0 + 4))
-
-    for h in range(2):
-        ts(A("Y0", 128 * h, 128 * h + 128), A("X0R", h, 256, 2), -1.0, OP.mult, 256.0, OP.add)
-    spread("Y0", 0, 8, "V")
-    spread("Y0", 8, 16, "S")
-    for h in range(2):
-        cp(A("A16", 128 * h, 128 * h + 128), A("P0R", h, 256, 2))
-    t32(A("C16"), A("A16"))
-    swap("sps", "C16")
-    SD = B(T.sps[:, 0:16, :], "sps", 0, 16)
-    ts(A("PFL"), SD, 2.0 ** -11, OP.mult)
-    offs("PO0")
-    ts(A("FS"), A("IF"), col(10), OP.is_equal, 32.0, OP.mult)
-
-    def pay0():
-        act(A("TA"), A("PFL"), bias=1.0)
-        act(A("TB"), A("PFL"), scale=2.0 ** -11)
-
-    def pay1(pa):
-        tt(A(pa, 1, 256), A("TA", 1, 256), A("TB", 0, 255), OP.add)
-
-    def pens(km):
-        tt(A("EQ"), A("PFL", 0, 128), A("PFL", 128, 256), OP.is_equal)
-        scan(A("PRE"), A("RES1", 0, 128), A("EQ"), OP.max, OP.min)
-        tt(A("PM"), A("PRE"), A("NEGM"), OP.mult)
-        tt(A(km), A("PM"), A("KRV0"), OP.add)
-
-    for j in range(4):
-        o, i = A("TX", 512 * j, 512 * j + 512), A("TXR", 512 * j, 512 * j + 512)
-        if j % 2 == 0:
-            ts(o, i, -1.0, OP.mult, 256.0, OP.add)
+            ts(A("SW", 128 * j, 128 * j + 128), A("IF", 0, 128), float(16 * (y - x)), OP.subtract, col(6 + x), OP.is_equal)
+    act(A("NID"), A("ID"), scale=-1.0)
+    act(A("ID64"), A("ID"), scale=64.0)
+    ts(A("FS"), A("IF"), col(9), OP.is_equal, 32.0, OP.mult)
+    act(A("FN"), A("FS"), scale=-1.0)
+    cp(A("IDH"), A("ID"))
+    ts(A("CF"), A("RES"), 0.0, OP.mult, -OFF, OP.add)
+    fill(A("EX1", 0, 128, 16), -2.0 ** 22)
+    for s in range(2):
+        fill(A("NE%d" % s), 0.0)
+        fill(A("BKA%d" % s), 2.0)
+        ts(A("BKB%d" % s), A("RES", 0, 128), 0.0, OP.mult)
+    ts(A("IU"), A("IF", 0, 128), col(10), OP.subtract, 1.0 / 32, OP.mult)
+    ts(A("IV"), A("IF", 0, 64), 2.0 ** -11, OP.mult, -63.0 / 4096, OP.add)
+    ts(A("BASE"), A("B0"), col(1), OP.add, 2.0 ** -11, OP.mult)
+    for u in range(32):
+        if u < 12:
+            keep(A("REP", 128 * u, 128 * u + 128), A("C256"), RPAT, OP.is_equal, 0.0, -u, 1)
         else:
-            act(o, i, scale=-1.0, bias=256.0)
-    WIN = A("TX", 0, 2048)
+            ts(A("REP", 128 * u, 128 * u + 128), A("RB"), float(u), OP.is_equal, 256.0, OP.mult)
 
-    def tables():
-        ts(A("BDM"), A("MG"), col(2), OP.is_equal)
-        ts(A("T1", 0, 128), A("MU"), 1.0, OP.add)
-        tt(A("T1", 128, 256), A("T1", 0, 128), A("BDM"), OP.mult)
-        ts(A("IU"), A("T1", 128, 256), -1.0, OP.add)
+    def one_set(s):
+        def a(n, lo=0, hi=None, st=1):
+            return A("%s%d" % (n, s), lo, hi, st)
 
-    def tables2():
-        ts(A("BD"), A("BDM"), -256.0, OP.mult)
-        ts(A("H16"), A("IF", 0, 16), col(1), OP.is_equal)
-        for u in range(16):
-            ts(A("REP", 128 * u, 128 * u + 128), A("BD"), A("H16", u, u + 1), OP.mult)
-        ts(A("O1"), A("BASE"), col(1), OP.add)
-        ts(A("BASE"), A("O1"), 2.0 ** -11, OP.mult)
+        def nd(n, *ix):
+            return N("%s%d" % (n, s), *ix)
 
-    def dist(off, ps, ex, hooks=()):
-        do("S", lambda: g.scalar.activation(T.TG[:], T.TX[:, 0:2048].indirect(T[off][:, 32:64]), AF.Copy, bias=0.0, scale=1.0),
-           [A("TG")], [WIN, A(off, 32, 64)])
-        mm(A("t3"), A("ID"), A("TG"), True, False)
-        mm(A("t3"), A("NID"), A("XR", 512, 1024), False, True)
-        for h in range(4):
-            lo, hi = 1024 * h, 1024 * h + 1024
-            m = hi if h else lo + 512
-            gat(A("DF", lo, m), WIN, A(off, lo // 16, m // 16), A("XR", 0, m - lo), OP.subtract)
-            if h < len(hooks):
-                hooks[h]()
-            out = A(ps, h, 256, 4)
-            st = (1, 2, 2, 4)[h]
-            n = 0
-            for b0 in range(st):
-                nm = "AD%d_%d" % (h, b0)
-                act(B(T.AD[:, lo + b0:m:st], nm, lo, m), B(T.DF[:, lo + b0:m:st], "DF", lo, m), AF.Abs)
-                if h == 0:
-                    act(B(T.AD[:, m:hi], nm, m, hi), A("t3"), AF.Abs)
-                for b in range(b0, 16, st):
-                    mm(out, A("FS", 15 - b, 143 - b), B(T.AD[:, lo + b:hi:16], nm, lo, hi), n == 0, n == 15)
-                    n += 1
-                    if n == (4 if h == 3 else 14):
-                        for c in (0, 128):
-                            mm(A(ps, c + h, c + 128, 4), A("ID"), A(ex, h, 128, 4), False, False)
+        SD, K, Z = nd("sp", slice(0, 8), ALL), a("k", 0, 128), a("k", 128, 256)
+        WIN, XR = a("TX", 0, W), a("TX", W, W + 512)
 
-    def latch(key, pay, res, o0, o1):
-        scan(A("FM"), A(res), key, o0, o1)
-        tt(A("RR"), key, A("FM"), OP.is_equal)
-        tt(A("D1"), pay, A("RR"), OP.subtract)
-        scan(A("LT"), A("RR"), A("D1"), OP.max, OP.min)
+        def swap(src):
+            for x in range(2):
+                for y in range(2):
+                    j = 2 * x + y
+                    mm(nd("sp", slice(x, 8, 2), ALL), A("SW", 128 * j, 128 * j + 128), nd(src, slice(y, 8, 2), ALL), y == 0, y == 1)
 
-    LAST = A("LT", 15, 256, 16)
-    FML = A("FM", 15, 256, 16)
-    DPS, EPS = A("dps", 0, 256), A("eps", 0, 256)
-    PAE = A("kps", 128, 384)
-    PAP = A("t2", 0, 256)
-    BGP = A("eps", 256, 512)
-    MPS = A("dps", 256, 384)
-    OH = A("dps", 256, 512)
-    PX = A("t0", 0, 256)
-    for r in range(NR):
-        last = r == NR - 1
-        Y, PO, KM, PA, MK, MS = ["%s%d" % (n, r) for n in ("Y", "PO", "KM", "PA", "MK", "MS")]
-        if r:
-            for n, s in ((Y, "ry"), (PO, "rp"), (KM, "rk"), (PA, "ra")):
-                land(A(n), "%s_%d" % (s, r), prv, [core])
-        if r:
-            spread(Y, 0, 8, "V")
-            spread(Y, 8, 16, "S")
-        else:
-            pay0()
-        dist(PO, "dps", KM, (lambda: pens("KM0"), tables, lambda: pay1("PA0")) if r == 0 else ())
-        act(A("TX", 2048, 2304), A(Y), AF.Copy)
-        act(PAP, A(PA), AF.Copy)
-        if r == 0:
-            act(A("RESB"), A("RES1"), scale=1048576.0)
-            act(BGP, A("BIGK"), AF.Copy)
-        else:
-            act(A("THA"), A(KM), AF.Relu, scale=-1.0)
+        def chain(r, lo=0, hi=128, st=1):
+            return a("RL", 256 * r + lo, 256 * r + hi, st)
+
+        def text(r):
+            return a("RL", 256 * r + 128, 256 * r + 256)
+
+        def small(j, n=1):
+            return a("SM", 8 * j, 8 * j + 8 * n)
+
+        def table(r, j):
+            return a("MK", 64 * (NG * r + j), 64 * (NG * r + j) + 64)
+
+        def first():
             for h in range(2):
-                act(A("THB", 128 * h, 128 * h + 128), A("THA"), scale=-1.0, bias=65536.0)
-        latch(DPS, PAP, "RES", OP.mult, OP.max)
-        ts(A("PAYI"), LAST, 4194304.0, OP.mult)
-        ts(A("UVI", 0, 16), A("PAYI"), 18, SHR)
-        ts(A("UVI", 16, 32), A("PAYI"), 11, SHR, 127, AND)
-        cp(A("UVF"), A("UVI"))
-        for c in range(16):
-            lo, hi = 128 * c, 128 * c + 128
-            ts(A("OU", lo, hi), A("IU"), A("UVF", c, c + 1), OP.is_equal)
-            ts(A("OV", lo, hi), A("IV"), A("UVF", 16 + c, 17 + c), OP.is_equal)
-            mm(MPS, A("OU", lo, hi), A("OV", lo, hi), c == 0, c == 15)
-        ts(A(MS), MPS, 0.5, OP.is_ge)
-        send(A(MS), rest(rank), T[MK][:, 128 * rank:128 * rank + 128], "mk%d_%d" % (r, rank))
-        for j in range(NG):
-            if j != rank:
-                land(A(MK, 128 * j, 128 * j + 128), "mk%d_%d" % (r, j), T.cores[j], rest(j))
-        if r:
-            tt(A("T1"), DPS, A("THB"), OP.is_ge)
-            tt(A("D1"), A("T1"), BGP, OP.mult)
-            tt(DPS, DPS, A("D1"), OP.max)
-            latch(DPS, PAP, "RES", OP.mult, OP.max)
-            ts(A("PAYI"), LAST, 4194304.0, OP.mult)
-        ts(A("TEI"), A("PAYI"), 2047, AND)
-        cp(A("TEO"), A("TEI"))
-        gat(A("A16"), A("PU"), A("TEO"))
-        t32(A("C16"), A("A16"))
-        swap("sps", "C16")
-        cp(A("DKI"), FML)
-        ts(A("PKI"), A("PAYI"), 11, SHR)
-        ts(A("DKJ"), A("DKI"), 15, AND)
-        ts(A("PK"), A("PKI"), 2.0 ** -11, OP.mult)
-        ts(A("DKM"), FML, 16.0, OP.subtract, 65536.0, OP.min)
-        cp(A("BKA", 0, 256, 16), A("DKJ"))
-        if r == 0:
-            tables2()
-        else:
-            for h in range(4):
-                ts(A("PFL", h, 256, 4), A(PO, 64 * h, 64 * h + 64), 2.0 ** -11, OP.mult)
-        scan(OH, A("RES"), A("BKA"), OP.mult, OP.add)
-        def bank(q, lo, hi):
-            return A("t%d" % q, lo, hi)
-        order = (3, 0, 2, 1)
-        for q in order:
-            mm(bank(q, 0, 512), A("ID"), A("TX", 512 * q, 512 * q + 512), True, False)
-        mm(A("kps", 0, 128), A("ID"), A(MS), True, False)
-        js = [j for j in range(NG) if j != rank]
-        for j in js:
-            mm(A("kps", 0, 128), A("ID"), A(MK, 128 * j, 128 * j + 128), False, j == js[-1])
-        ts(A("CUT"), A("kps", 0, 128), 3.5, OP.is_ge)
-        for q in order:
-            for u in range(4):
-                v = 4 * q + u
-                mm(bank(q, 128 * u, 128 * u + 128), A("REP", 128 * v, 128 * v + 128), A("CUT"), False, u == 3)
-        for h in range(4):
-            cp(A("PDO", 64 * h, 64 * h + 64), B(T.sps[:, 0:16, h:16:4], "sps", 0, 16))
-        for n, q in enumerate(order):
-            o = A("TX", 512 * q, 512 * q + 512)
-            if n % 2 == 0:
-                ts(o, bank(q, 0, 512), 0.0, OP.max)
-                if n == 0:
-                    tt(OH, OH, A("KREV"), OP.is_equal)
+                ts(a("A16", 64 * h, 64 * h + 64), a("P0R", h, 128, 2), 2.0 ** -11, OP.mult)
+                ts(a("RL", 128 + 64 * h, 192 + 64 * h), a("X0R", h, 128, 2), XO, OP.add)
+            t32(nd("C16", ALL, ALL), a("A16"))
+            swap("C16")
+            cp(chain(0), SD)
+
+        def prep(r):
+            for h in (1, 3, 0, 2):
+                ts(a("PO", 32 * h, 32 * h + 32), chain(r, h, 128, 4), 2048.0, OP.mult)
+            if SPREAD == "V":
+                for l in range(2):
+                    ts(nd("XQ", ALL, l, ALL), text(r), XO, OP.subtract)
+                cp(nd("XQ", ALL, slice(2, 4), ALL), nd("XQ", ALL, slice(0, 2), ALL))
+                cp(XR, nd("XQ", ALL, ALL, ALL))
             else:
-                act(o, bank(q, 0, 512), AF.Relu)
-        dist("PDO", "eps", "KFW")
-        if r == 0:
-            cp(A("CAC"), A("CUT"))
-        else:
-            tt(A("CA2" if r == 1 else "CAC"), A("CAC" if r == 1 else "CA2"), A("CUT"), OP.max)
-        ts(PAE, SD, 2.0 ** -11, OP.mult, 1.0, OP.add)
-        tt(PX, OH, A("PFL"), OP.mult)
-        tt(A("PZ"), A("PFL"), PX, OP.subtract)
-        latch(EPS, PAE, "RESB", OP.add, OP.min)
-        tt(A("O1"), LAST, A("BASE"), OP.subtract)
-        tt(A("TK"), A("DKM"), FML, OP.is_ge)
-        tt(A("N1"), LAST, A("PK"), OP.subtract)
-        tt(A("O2"), A("O1"), A("TK"), OP.mult)
-        tt(A("N2"), A("N1"), A("TK"), OP.mult)
-        tt(A("OF"), A("O2"), A("BASE"), OP.add)
-        tt(A("BKB", 0, 256, 16), A("N2"), A("PK"), OP.add)
-        ts(A("OFO"), A("OF"), 2048.0, OP.mult)
-        gat(A("SU"), A("TX"), A("OFO"), A(Y), OP.add)
-        e = r + 1
-        YS = "YS%d" % e
-        act(A(YS), A("SU"), scale=0.5, bias=0.25)
-        if not last:
-            send(A(YS), [nxt], T["Y%d" % e][:], "ry_%d" % e)
-        NB, NV = A("T1"), A("t0", 256, 512)
-        scan(NB, A("RES"), A("BKB"), OP.mult, OP.add)
-        tt(NV, OH, NB, OP.mult)
-        if not last:
-            tt(A("PFL"), A("PZ"), NV, OP.add)
-            offs("POS%d" % e)
-            send(A("POS%d" % e), [nxt], T["PO%d" % e][:], "rp_%d" % e)
-            pay0()
-            pens("KMS%d" % e)
-            pay1("PAS%d" % e)
-            send(A("KMS%d" % e), [nxt], T["KM%d" % e][:], "rk_%d" % e)
-            send(A("PAS%d" % e), [nxt], T["PA%d" % e][:], "ra_%d" % e)
-        else:
-            tt(A("PNH"), A("PZ"), NV, OP.add)
-            swap("sps", "PNH")
+                for l in range(4):
+                    mm(nd("sp", slice(l, 32, 4), ALL), A("IDH"), text(r), l == 0, l == 3)
+                if SPREAD == "S":
+                    act(XR, nd("sp", ALL, ALL), bias=-XO)
+                else:
+                    ts(XR, nd("sp", ALL, ALL), XO, OP.subtract)
+            tt(a("NE", 1, 64), chain(r, 0, 63), chain(r, 64, 127), OP.not_equal)
             for h in range(2):
-                act(A("YXB", h, 256, 2), A(YS, 128 * h, 128 * h + 128), scale=-1.0, bias=256.0)
-            store("Y", T.yx[:], A("YXB"), "oyx")
-            store("Y", T.yc[:], A("CAC"), "oyc")
-            t32(A("YPA"), SD)
-            ts(A("YPB", 0, 256, 2), A("YPA", 0, 128), 2048.0, OP.mult)
-            act(A("YPB", 1, 256, 2), A("YPA", 128, 256), scale=2048.0)
-            store("Y", T.yp[:], A("YPB"), "oyp")
+                scan(a("RQ", 64 * h, 64 * h + 64), a("NE"), A("RES", 0, 64), OP.max, OP.min)
+            mm(Z, A("IDH"), A("CF", 0, 128), True, False)
+            mm(Z, A("ID"), A("KA"), False, False)
+            mm(Z, A("IDH"), chain(r), False, True)
 
-    for s in ["oyp", "oyx", "oyc"] + LOADS:
-        g.sync.wait_ge(T.sem[s], 16)
+        def sums(e, ex, lin):
+            out = a("k", e, 128, 2)
+            mm(out, A("ID"), A(ex, e, 128, 2), True, False)
+            for h in lin:
+                for b in range(16):
+                    mm(a("k", h, 128, 4), A("FN", 15 - b, 143 - b), a("DF", 512 * h + b, 512 * h + 512, 16), False, False)
+            for b in list(range(0, 16, 2)) + list(range(1, 16, 2)):
+                mm(out, A("FS", 15 - b, 143 - b), nd("AD", ALL, slice(e, 16, 2), b), False, b == 15)
+
+        def dist(off, ex, who):
+            bank = 0
+            for h, q in zip((1, 3, 0, 2), who):
+                o = a(off, 32 * h, 32 * h + 32)
+                if q != "S":
+                    src, lo = "DF", 512 * h
+                    gat(a(src, lo, lo + 512), WIN, o, XR, OP.subtract)
+                else:
+                    src, lo = ("ta", "tb")[bank % 2], 0
+                    bank += 1
+                    act(a("TG", 512 * h, 512 * h + 512), WIN, AF.Copy, off=o)
+                    mm(a(src), A("NID"), nd("XQ", ALL, ALL, ALL) if SPREAD == "V" else XR, True, False)
+                    mm(a(src), A("ID"), a("TG", 512 * h, 512 * h + 512), False, True)
+                if q == "R":
+                    ts(nd("AD", ALL, slice(h, 16, 4), ALL), a(src, lo, lo + 512), 0.0, OP.max, 2.0, OP.mult)
+                else:
+                    st = 2 if h == 2 + PARITY[1] else 1
+                    for b0 in range(st):
+                        act(nd("AD", ALL, slice(h, 16, 4), slice(b0, 16, st)), a(src, lo + b0, lo + 512, st), AF.Abs)
+            for e in PARITY:
+                sums(e, ex, [h for h, q in zip((1, 3, 0, 2), who) if q == "R" and h % 2 == e])
+
+        def charges(r):
+            scan(a("FM"), a("RQ"), K, OP.mult, OP.max)
+            tt(a("NR"), K, a("FM"), OP.not_equal)
+            scan(a("LL", 0, 128), a("NR"), Z, OP.mult, OP.max)
+            last = a("LL", 15, 128, 16)
+            ts(small(0), last, M2, OP.add, M2, OP.subtract)
+            ts(small(1), last, M32, OP.add, M32, OP.subtract)
+            mps = nd("sp", slice(16, 20), ALL)
+            for c in range(8):
+                ou, ov = a("OU", 128 * c, 128 * c + 128), a("OV", 64 * c, 64 * c + 64)
+                kk, hh = a("SM", c, c + 1), a("SM", 8 + c, 9 + c)
+                ts(ou, A("IU"), kk, OP.add, hh, OP.is_equal)
+                ts(ov, A("IV"), hh, OP.add, a("LL", 16 * c + 15, 16 * c + 16), OP.is_equal)
+                mm(mps, ou, ov, c == 0, c == 7)
+            ms = table(r, rank)
+            ts(ms, mps, 0.5, OP.is_ge)
+            send([(ms, ms, d, e) for d, e in spread_plan(core)], "mk%d_%d" % (s, r), [table(r, j) for j in range(NG) if j != rank],
+                 sum(len(e) for c in T.cores if c != core for d, e in spread_plan(c) if core in d), TABLES)
+
+        def teach(r):
+            zk, zt = a("LL", 15, 128, 16), a("LL", 143, 256, 16)
+            if r:
+                act(a("SG"), K, AF.Sign, bias=0.5 - CUTKEY)
+                mm(a("k", 256, 512), A("IDH"), A("CF"), True, False)
+                mm(a("k", 256, 512), A("ID"), A("KG"), False, False)
+                mm(a("k", 256, 384), A("IDH"), chain(r), False, False)
+                mm(a("k", 385, 512), A("IDH"), chain(r, 0, 127), False, False)
+                mm(a("k", 256, 384), A("ID64"), a("SG"), False, False)
+                mm(a("k", 384, 512), A("ID64"), a("SG"), False, True)
+            scan(a("LL", 129, 256), a("NR", 1, 128), a("k", 128, 255), OP.mult, OP.max)
+            if r:
+                scan(a("GL"), A("RES"), a("k", 256, 512), OP.mult, OP.max)
+                tt(small(2, 2), a("GL", 15, 256, 16), a("LL", 15, 256, 16), OP.max)
+                ts(small(7), a("FM", 15, 128, 16), CUTKEY, OP.min)
+                ts(small(8), a("GL", 15, 128, 16), CUTKEY, OP.mult, CUTKEY, OP.min)
+                tt(small(9), small(7), small(8), OP.max)
+                zk, zt = small(2), small(3)
+            kk = a("BKA", 0, 128, 16)
+            ts(kk, zk, M2, OP.add, M2 + 32, OP.subtract)
+            tt(small(5), zt, kk, OP.subtract)
+            tt(small(4), zk, kk, OP.subtract)
+            ts(a("TEO"), small(5), 2048.0, OP.mult, 2048 * (OFF - 34), OP.add)
+            ts(small(6), small(4), OFF - 32, OP.add)
+            gat(a("A16"), a("PU"), a("TEO"), 2.0 ** -11, OP.mult)
+            t32(nd("C16", ALL, ALL), a("A16"))
+            swap("C16")
+            for h in (1, 3, 0, 2):
+                ts(a("PD", 32 * h, 32 * h + 32), nd("sp", slice(0, 8), slice(h, 16, 4)), 2048.0, OP.mult)
+            scan(a("OS"), A("RES", 0, 128), a("BKA"), OP.mult, OP.add)
+            ts(a("OH"), a("OS"), 0.0, OP.is_equal)
+
+        def cuts(r):
+            mine = [q for q in range(4) if QUARTERS[q] == "S"]
+            banks = [("ta", "tb", "k", "ta")[mine.index(q)] if q in mine else "k" for q in range(4)]
+            if len(mine) == 3:
+                banks[mine[2]] = "ta"
+            for q in mine[:2]:
+                mm(a(banks[q]), A("ID"), a("TX", 512 * q, 512 * q + 512), True, False)
+            sm, ct = a("k", 256, 320), a("CT", 64 * r, 64 * r + 64)
+            js = [rank] + [j for j in range(NG) if j != rank]
+            for j in js:
+                mm(sm, A("ID"), table(r, j), j == js[0], j == js[-1])
+            act(ct, sm, AF.Relu, bias=-3.0)
+            for q in range(4):
+                tx, b = a("TX", 512 * q, 512 * q + 512), a(banks[q])
+                if q in mine[2:]:
+                    mm(b, A("ID"), tx, True, False)
+                for u in range(8):
+                    v = 8 * q + u
+                    j = mm(a(banks[q], 64 * u, 64 * u + 64), A("REP", 128 * v, 128 * v + 128), ct, u == 0 and QUARTERS[q] == "V", u == 7,
+                           (j, 0.0) if v else None)
+                if QUARTERS[q] == "S":
+                    act(tx, b, AF.Copy)
+                else:
+                    tt(tx, b, tx, OP.add)
+            if r == NR - 1:
+                o = nd("sp", slice(20, 24), ALL)
+                for j in range(NR):
+                    mm(o, A("ID"), a("CT", 64 * j, 64 * j + 64), j == 0, j == NR - 1)
+                act(a("YC"), o, AF.Sign)
+                put("Y", lambda: g.sync.dma_start(T.yc[4 * s:4 * s + 4, :], a("YC")[0]).then_inc(T.sem["oyc%d" % s], 16), [], [a("YC")], 0.05, ("", 0))
+
+        def replace(r):
+            last, NB, NV = a("L3", 15, 128, 16), a("k", 256, 384), a("k", 384, 512)
+            xd, x, tk, of, n1 = [small(j) for j in range(10, 15)]
+            scan(a("F3"), A("RESB"), K, OP.add, OP.min)
+            tt(a("NR"), K, a("F3"), OP.not_equal)
+            tt(xd, a("F3", 15, 128, 16), small(9) if r else a("FM", 15, 128, 16), OP.subtract)
+            tt(a("D1"), SD, a("NR"), OP.subtract)
+            tt(x, xd, A("BASE"), OP.min)
+            scan(a("L3"), a("NR"), a("D1"), OP.mult, OP.max)
+            ts(tk, xd, 0.0, OP.is_le)
+            tt(of, x, last, OP.max)
+            tt(n1, last, small(6), OP.subtract)
+            ts(a("OFO"), of, 2048.0, OP.mult)
+            tt(a("BKB", 0, 128, 16), n1, tk, OP.mult)
+            gat(a("SU"), a("TX"), a("OFO"), text(r), OP.add)
+            scan(NB, A("RES", 0, 128), a("BKB"), OP.mult, OP.add)
+            ps, xs = a("RS", 256 * r, 256 * r + 128), a("RS", 256 * r + 128, 256 * r + 256)
+            ts(xs, a("SU"), 0.5, OP.mult, XO / 2 - 0.25, OP.add)
+            tt(NV, NB, a("OH"), OP.mult)
+            if r + 1 < NR:
+                tt(ps, NV, chain(r), OP.add)
+                there = chain(r + 1, 0, 256)
+                send([(a("RS", 256 * r, 256 * r + 256), there, [nxt], pow2(common(core, [nxt])))], "rg%d_%d" % (s, r + 1),
+                     [there], len(pow2(common(prv, [core]))), RING)
+            else:
+                tt(nd("PN", ALL, ALL), NV, chain(r), OP.add)
+                swap("PN")
+                for h in range(2):
+                    ts(a("YX", h, 128, 2), a("RS", 256 * r + 128 + 64 * h, 256 * r + 192 + 64 * h), XO, OP.subtract)
+                store("SS", T.yx, "YX%d" % s, s, "oyx%d" % s)
+                t32(a("YPA"), SD)
+                for h in range(2):
+                    ts(a("YP", h, 128, 2), a("YPA", 64 * h, 64 * h + 64), 2048.0, OP.mult)
+                store("YS", T.yp, "YP%d" % s, s, "oyp%d" % s)
+
+        first()
+        for r in range(NR):
+            prep(r)
+            dist("PO", "EX1", CHAINS)
+            charges(r)
+            teach(r)
+            cuts(r)
+            dist("PD", "EX2", PUPILS)
+            replace(r)
+
+    for s in range(2):
+        now[0] = s
+        one_set(s)
+    cnt = issue()
+
+    for s in STORES + LOADS:
+        g.sync.wait_ge(T.sem[s], 16 if s[1:3] == "yc" else 32)
     g.wait_ge(T.sem.loc, sent[0])
     for q in ("V", "S", "P", "G"):
         g.wait_ge(T.sem[SEM[q]], cnt[q])

import numpy as np
from concourse.bass import DstId, RemoteDMATransfer
from concourse.mybir import AluOpType as OP, ActivationFunctionType as AF

NR = 3
STEP = 5
NG = 8
W = 2048
CUTKEY = 65536.0
M2, M32 = 1.5 * 2 ** 24, 1.5 * 2 ** 18
OFF = 991.5 / 2048
XO = 1536.0

F4, BF, HF, I4, U2 = "float32", "bfloat16", "float16", "int32", "uint16"
SCRATCH = {}
for _n, _w, _d in (
        ("PI", 8, I4), ("PF", 12, F4), ("IF", 144, F4), ("FS", 144, BF), ("FN", 144, BF), ("ID", 128, BF), ("NID", 128, BF), ("ID64", 128, BF), ("IDH", 128, HF),
        ("SW", 512, HF), ("CF", 256, HF), ("KA", 128, BF), ("KG", 256, BF), ("EX1", 128, BF), ("EX2", 128, BF), ("RES", 256, BF), ("RESB", 128, BF),
        ("IU", 128, BF), ("IV", 64, BF), ("RB", 128, BF), ("C256", 128, BF), ("REP", 4096, BF), ("B0", 8, F4), ("BASE", 8, F4)):
    SCRATCH[_n] = ("sbuf", [128, _w], _d)
for _s in range(2):
    for _n, _w, _d in (
            ("TX", W + 512, BF), ("PU", W, I4), ("P0R", 128, I4), ("X0R", 128, BF), ("RL", 256 * NR, HF), ("RS", 256 * NR, HF),
            ("PO", 128, U2), ("PD", 128, U2), ("RQ", 128, BF), ("NE", 64, BF), ("FM", 128, F4), ("NR", 128, BF),
            ("LL", 256, F4), ("GL", 256, F4), ("SG", 128, BF), ("SM", 128, F4), ("TEO", 8, U2), ("OFO", 8, U2), ("BKA", 128, BF), ("BKB", 128, HF),
            ("OH", 128, BF), ("MK", 64 * NG * NR, BF), ("CT", 64 * NR, BF), ("YC", 64, F4), ("YP", 128, F4), ("YX", 128, BF),
            ("DF", 2048, BF), ("TG", 2048, BF), ("OU", 1024, BF), ("OV", 512, BF), ("A16", 128, HF), ("D1", 128, F4), ("F3", 128, F4),
            ("L3", 128, F4), ("OS", 128, BF), ("SU", 128, HF), ("YPA", 128, F4)):
        SCRATCH["%s%d" % (_n, _s)] = ("sbuf", [128, _w], _d)
    SCRATCH["XQ%d" % _s] = ("sbuf", [128, 8, 4, 16], BF)
    SCRATCH["AD%d" % _s] = ("sbuf", [128, 8, 16, 16], BF)
    for _n in ("PN", "C16"):
        SCRATCH["%s%d" % (_n, _s)] = ("sbuf", [128, 8, 16], HF)
    SCRATCH["sp%d" % _s] = ("psum", [128, 32, 16], F4)
    for _n in ("k", "ta", "tb"):
        SCRATCH["%s%d" % (_n, _s)] = ("psum", [128, 512], F4)
PSUM = [n for n in SCRATCH if SCRATCH[n][0] == "psum"]

LOADS = ["l%s%d" % (n, s) for s in range(2) for n in ("p0", "x0", "tx", "pu")]
STORES = ["o%s%d" % (n, s) for s in range(2) for n in ("yp", "yx", "yc")]
SEMAPHORES = (["qv", "qs", "qp", "qg", "loc"] + LOADS + STORES + ["mk%d_%d" % (s, r) for s in range(2) for r in range(NR)]
              + ["rg%d_%d" % (s, r) for s in range(2) for r in range(1, NR)])

CHAINS, PUPILS, QUARTERS, SPREAD, PARITY = "SSRR", "SSRR", "SVSS", "S", (0, 1)
CYCLE, PECYCLE, GATHER, WAKE = 1.04e-3, 0.52e-3, 1.56, 0.07
TABLES, RING, FIRST = 5.5, 4.2, 2.8
ARRIVE = {"lp00": 2.2, "lx00": 2.5, "ltx0": 4.8, "lp01": 5.3, "lx01": 5.7, "ltx1": 8.8, "lpu0": 14.0, "lpu1": 20.0}
LEAD = 8.0
ORDER, MASKS = [], {}


def place(ops, order, deps, at):
    start, busy = {}, {}
    for i in order:
        o = ops[i]
        t = max([at[i]] + [start[j] + ops[j]["dur"] + lat for j, lat in deps[i].items() if j in start])
        if o["dur"]:
            line = busy.setdefault(o["q"], [])
            n = 0
            while n < len(line) and line[n][0] < t + o["dur"]:
                t = max(t, line[n][1])
                n += 1
            line.insert(n, (t, t + o["dur"]))
        start[i] = t
    return start


def improve(ops, order, fw, bw, passes):
    for it in range(passes):
        st = place(ops, order, fw, [o["at"] for o in ops])
        back = place(ops, sorted(order, key=lambda i: (-st[i] - ops[i]["dur"], -i)), bw, [0.0] * len(ops))
        order = sorted(order, key=lambda i: (-back[i] - ops[i]["dur"], i))
    return st, back


def issue_order(ops):
    n = len(ops)
    fw, bw = [o["deps"] for o in ops], [{} for o in ops]
    way = [0.0] * n
    for i in range(n - 1, -1, -1):
        way[i] += ops[i]["dur"]
        for j, lat in fw[i].items():
            bw[j][i] = lat
            way[j] = max(way[j], way[i] + lat)
    m = sum(o["set"] for o in ops)
    one = sorted(range(n - m), key=lambda i: (-way[i], i))
    st, back = improve(ops, one, fw, bw, 2)
    late = {i: -back[i] - ops[i]["dur"] for i in one}
    for i in range(n - m, n):
        late[i] = late[i - m] + LEAD
    for i in range(n - 1, -1, -1):
        for j in fw[i]:
            late[j] = min(late[j], late[i])
    st, back = improve(ops, sorted(range(n), key=lambda i: (late[i], i)), fw, bw, 2)
    return sorted(range(n), key=lambda i: (st[i], i))


def rank_program(g, core, T, topo):
    rank = T.rank_of(core)
    if rank is None:
        return
    Q = {"V": g.vector, "S": g.scalar, "P": g.tensor, "G": g, "Y": g.sync}
    SEM = {"V": "qv", "S": "qs", "P": "qp", "G": "qg"}
    ALL = slice(None)
    masks = MASKS
    sent = [0]

    def N(n, *ix):
        key = (n, repr(ix))
        if key not in masks:
            m = np.zeros(SCRATCH[n][1][1:], np.uint8)
            m[ix] = 1
            masks[key] = (int.from_bytes(np.packbits(m.reshape(-1), bitorder="little").tobytes(), "little"), int(m.sum()))
        return (T[n][(ALL,) + ix], n) + masks[key]

    def A(n, lo=0, hi=None, st=1):
        hi = SCRATCH[n][1][1] if hi is None else hi
        return N(n, slice(lo, hi) if st == 1 else slice(lo, hi, st))

    def clash(q, isw, n, m, e):
        return (n in PSUM and e[2] != q) or ((isw or e[1]) and m & e[0])

    ops, seen, now = [], {}, [0]

    def put(q, f, outs, ins, dur, sem=None, at=0.0, after=None):
        deps = dict([after]) if after else {}
        for isw, xs in ((False, ins), (True, outs)):
            for (_, n, m, _c) in xs:
                for e in seen.get(n, ()):
                    if q == e[2] == "P" and n in PSUM:
                        deps[e[3]] = 0.0
                    elif clash(q, isw, n, m, e):
                        deps[e[3]] = WAKE
        for (_, n, m, _c) in outs:
            seen[n] = [e for e in seen.get(n, []) if (e[2] == q or n not in PSUM) and e[0] & ~m] + [(m, True, q, len(ops))]
        for (_, n, m, _c) in ins:
            seen.setdefault(n, []).append((m, False, q, len(ops)))
        ops.append({"q": q, "f": f, "outs": outs, "ins": ins, "dur": dur, "sem": sem, "at": at, "deps": deps, "set": now[0]})
        return len(ops) - 1

    def issue():
        cnt = {q: 0 for q in SEM}
        known = {q: {} for q in Q}
        past, acc = {}, {}
        if not ORDER:
            ORDER.extend(issue_order(ops))
        for o in [ops[i] for i in ORDER]:
            q, w = o["q"], {}
            if q in Q:
                for isw, xs in ((False, o["ins"]), (True, o["outs"] if o["sem"] is None else [])):
                    for (_, n, m, _c) in xs:
                        for e in acc.get(n, ()):
                            if not (q == e[2] == "P" and n in PSUM) and clash(q, isw, n, m, e) and known[q].get(e[3], 0) < e[4]:
                                w[e[3]] = max(w.get(e[3], 0), e[4])
                for s in sorted(w, key=lambda s: -len(past.get((s, w[s]), ()))):
                    if known[q].get(s, 0) < w[s]:
                        Q[q].wait_ge(T.sem[s], w[s])
                        known[q][s] = w[s]
                        for s2, v2 in past.get((s, w[s]), {}).items():
                            known[q][s2] = max(known[q].get(s2, 0), v2)
            if o["sem"] is None:
                o["f"]().then_inc(T.sem[SEM[q]], 1)
                cnt[q] += 1
                s, v = SEM[q], cnt[q]
                past[(s, v)] = dict(known[q])
            else:
                if o["f"]:
                    o["f"]()
                s, v = o["sem"]
                if not v:
                    continue
            for (_, n, m, _c) in o["outs"]:
                acc[n] = [e for e in acc.get(n, []) if (e[2] == q or n not in PSUM) and e[0] & ~m] + [(m, True, q, s, v)]
            for (_, n, m, _c) in o["ins"]:
                acc[n] = [e for e in acc.get(n, []) if not (e[0] == m and not e[1] and e[3] == s)] + [(m, False, q, s, v)]
        return cnt

    def vec(f, o, ins, k=None, extra=()):
        if k is None:
            k = 0.5 if all(SCRATCH[x[1]][2] in (BF, HF, U2) for x in [o] + ins) else 1
        put("V", f, [o], ins + list(extra), 0.03 + max(64, k * o[3]) * CYCLE)

    def cp(o, i):
        vec(lambda: g.vector.tensor_copy(o[0], i[0]), o, [i])

    def fill(o, v):
        vec(lambda: g.vector.memset(o[0], v), o, [])

    def tt(o, a, b, op):
        vec(lambda: g.vector.tensor_tensor(o[0], a[0], b[0], op), o, [a, b], 1 if a[1] in PSUM or b[1] in PSUM else 2)

    def ts(o, a, s1, op0, s2=None, op1=None):
        extra = [s for s in (s1, s2) if isinstance(s, tuple)]
        v1 = s1[0] if isinstance(s1, tuple) else s1
        v2 = s2[0] if isinstance(s2, tuple) else s2
        if op1 is None:
            vec(lambda: g.vector.tensor_scalar(o[0], a[0], v1, None, op0), o, [a], None, extra)
        else:
            vec(lambda: g.vector.tensor_scalar(o[0], a[0], v1, v2, op0, op1), o, [a], None, extra)

    def scan(o, d0, d1, op0, op1):
        vec(lambda: g.vector.tensor_tensor_scan(o[0], d0[0], d1[0], 0.0, op0, op1), o, [d0, d1])

    def t32(o, i):
        vec(lambda: g.vector.transpose(o[0], i[0]), o, [i])

    def gat(o, win, off, in1, op):
        ap = win[0].indirect(off[0])
        if isinstance(in1, tuple):
            vec(lambda: g.vector.tensor_tensor(o[0], ap, in1[0], op), o, [win, off, in1], GATHER)
        else:
            vec(lambda: g.vector.tensor_scalar(o[0], ap, in1, None, op), o, [win, off], GATHER)

    def act(o, i, func=AF.Identity, scale=1.0, bias=0.0, off=None):
        ap = i[0].indirect(off[0]) if off else i[0]
        put("S", lambda: g.scalar.activation(o[0], ap, func, bias=bias, scale=scale), [o], [i, off] if off else [i],
            0.06 + max(64, o[3] * (GATHER if off else 1)) * CYCLE)

    def mm(o, l, r, start, stop, after=None):
        return put("P", lambda: g.tensor.matmul(o[0], l[0], r[0], start, stop), [o], [l, r], max(64, o[3]) * PECYCLE, after=after)

    def iota(o, pat, base, cm):
        if SCRATCH[o[1]][2] == I4:
            put("G", lambda: g.iota(o[0], pat, base, cm), [o], [], 0.13)
        else:
            put("G", lambda: g.iota(o[0], pat, base, cm, allow_small_or_imprecise_dtypes=True), [o], [], 0.13 + 2 * o[3] * CYCLE)

    def keep(o, i, pat, cmp, fillv, base, cm):
        put("G", lambda: g.affine_select(o[0], i[0], pat, cmp, fillv, base, cm), [o], [i], 0.17 + 2 * o[3] * CYCLE)

    def load(qs, n, s, src, w, sem, after=None):
        for d in range(2):
            if after:
                Q[qs[d]].wait_ge(T.sem[after], 32)
            rows = src[64 * s:64 * s + 64, :] if w == W else src[64 * s:64 * s + 64, w * d:w * d + w]
            Q[qs[d]].dma_start(T[n][64 * d:64 * d + 64, 0:w], rows).then_inc(T.sem[sem], 16)
        put("R", None, [A(n, 0, w)], [], 0.0, (sem, 32), ARRIVE[sem])

    def store(qs, dst, n, s, sem):
        for d in range(2):
            put(qs[d], lambda d=d: Q[qs[d]].dma_start(dst[64 * s:64 * s + 64, 128 * d:128 * d + 128],
                                                      T[n][64 * d:64 * d + 64, :]).then_inc(T.sem[sem], 16), [], [A(n)], 0.05, (sem, 0))

    def pow2(e):
        n = 1
        while 2 * n <= len(e):
            n *= 2
        return e[:n]

    def common(src, dsts):
        return [x for x in topo.engines(src, dsts[0]) if all(x in topo.engines(src, d) for d in dsts)]

    def spread_plan(src):
        near = [c for c in T.cores if c != src and c in topo.cores_of(src)]
        far = [c for c in T.cores if c not in topo.cores_of(src)]
        ef = pow2(common(src, far))
        return [(far, ef), (near, pow2([x for x in common(src, near) if x not in ef]))]

    def send(parts, sem, lands, count, lat):
        trs = []
        for i, out, dsts, e in parts:
            ids = [DstId(rid=topo.addr(d, core)[0], pnc=topo.addr(d, core)[1]) for d in dsts]
            trs.append(RemoteDMATransfer(dst_ids=ids, dma_engine_mask=sum(1 << x for x in e), remote_sem=T.sem[sem],
                                         srcs=[i[0]], dsts=[out[0] for d in dsts]))
        lat += 0.0 if sent[0] else FIRST
        sent[0] += sum(len(p[3]) for p in parts)
        j = put("G", lambda: g.remote_dma_fused(trs, local_sem=T.sem.loc), [], [p[0] for p in parts], 0.9, (sem, 0))
        put("R", None, lands, [], 0.0, (sem, count), 0.0, (j, lat - 0.9))

    nxt = T.cores[(rank + STEP) % NG]
    prv = T.cores[(rank - STEP) % NG]

    load("YS", "P0R0", 0, T.p0, 128, "lp00")
    load("YS", "X0R0", 0, T.x0, 128, "lx00")
    load("YS", "TX0", 0, T.tx, W, "ltx0")
    load("YY", "P0R1", 1, T.p0, 128, "lp01")
    load("YY", "X0R1", 1, T.x0, 128, "lx01")
    load("YY", "TX1", 1, T.tx, W, "ltx1", "ltx0")
    load("YY", "PU0", 0, T.pu, W, "lpu0", "ltx1")
    load("YY", "PU1", 1, T.pu, W, "lpu1", "lpu0")

    def col(j):
        return A("PF", j, j + 1)

    iota(A("PI", 0, 1), [[0, 1]], 0, 1)
    iota(A("IF"), [[1, 144]], 0, 0)
    iota(A("KA"), [[0, 8], [-2, 16]], 32, 0)
    iota(A("EX1"), [[0, 8], [-1, 16]], 15, 0)
    iota(A("EX2"), [[0, 8], [1, 16]], 17, 0)
    iota(A("B0"), [[64, 8]], W, 0)
    RPAT = [[0, 2], [-32, 4], [0, 16]]
    iota(A("RB"), RPAT, 0, 1)
    for h in range(2):
        iota(A("KG", 128 * h, 128 * h + 128), [[0, 8], [-2, 16]], 2 * h - 32, 0)
    AND, SHR = OP.bitwise_and, OP.arith_shift_right
    ts(A("PI", 1, 2), A("PI", 0, 1), 15, AND)
    ts(A("PI", 2, 3), A("PI", 0, 1), 48, AND)
    ts(A("PI", 3, 4), A("PI", 0, 1), 4, SHR, 1, AND)
    ts(A("PI", 4, 5), A("PI", 0, 1), 112, AND)
    fill(A("RES"), 1.0)
    fill(A("RESB"), 0.0)
    fill(A("C256"), 256.0)
    cp(A("PF", 0, 5), A("PI", 0, 5))
    fill(A("RES", 0, 256, 16), 0.0)
    fill(A("RESB", 0, 128, 16), 2.0 ** 22)
    ts(col(6), col(3), -1000.0, OP.mult, col(0), OP.add)
    ts(col(8), col(3), 1000.0, OP.mult, -1000.0, OP.add)
    ts(col(9), col(4), 15.0, OP.add)
    ts(col(10), col(2), 2.0, OP.mult, 15.0, OP.add)
    ts(col(7), col(8), col(0), OP.add)
    ts(A("ID"), A("IF", 0, 128), col(0), OP.is_equal)
    for x in range(2):
        for y in range(2):
            j = 2 * x + y
            ts(A("SW", 128 * j, 128 * j + 128), A("IF", 0, 128), float(16 * (y - x)), OP.subtract, col(6 + x), OP.is_equal)
    act(A("NID"), A("ID"), scale=-1.0)
    act(A("ID64"), A("ID"), scale=64.0)
    ts(A("FS"), A("IF"), col(9), OP.is_equal, 32.0, OP.mult)
    act(A("FN"), A("FS"), scale=-1.0)
    cp(A("IDH"), A("ID"))
    ts(A("CF"), A("RES"), 0.0, OP.mult, -OFF, OP.add)
    fill(A("EX1", 0, 128, 16), -2.0 ** 22)
    for s in range(2):
        fill(A("NE%d" % s), 0.0)
        fill(A("BKA%d" % s), 2.0)
        ts(A("BKB%d" % s), A("RES", 0, 128), 0.0, OP.mult)
    ts(A("IU"), A("IF", 0, 128), col(10), OP.subtract, 1.0 / 32, OP.mult)
    ts(A("IV"), A("IF", 0, 64), 2.0 ** -11, OP.mult, -63.0 / 4096, OP.add)
    ts(A("BASE"), A("B0"), col(1), OP.add, 2.0 ** -11, OP.mult)
    for u in range(32):
        if u < 12:
            keep(A("REP", 128 * u, 128 * u + 128), A("C256"), RPAT, OP.is_equal, 0.0, -u, 1)
        else:
            ts(A("REP", 128 * u, 128 * u + 128), A("RB"), float(u), OP.is_equal, 256.0, OP.mult)

    def one_set(s):
        def a(n, lo=0, hi=None, st=1):
            return A("%s%d" % (n, s), lo, hi, st)

        def nd(n, *ix):
            return N("%s%d" % (n, s), *ix)

        SD, K, Z = nd("sp", slice(0, 8), ALL), a("k", 0, 128), a("k", 128, 256)
        WIN, XR = a("TX", 0, W), a("TX", W, W + 512)

        def swap(src):
            for x in range(2):
                for y in range(2):
                    j = 2 * x + y
                    mm(nd("sp", slice(x, 8, 2), ALL), A("SW", 128 * j, 128 * j + 128), nd(src, slice(y, 8, 2), ALL), y == 0, y == 1)

        def chain(r, lo=0, hi=128, st=1):
            return a("RL", 256 * r + lo, 256 * r + hi, st)

        def text(r):
            return a("RL", 256 * r + 128, 256 * r + 256)

        def small(j, n=1):
            return a("SM", 8 * j, 8 * j + 8 * n)

        def table(r, j):
            return a("MK", 64 * (NG * r + j), 64 * (NG * r + j) + 64)

        def first():
            for h in range(2):
                ts(a("A16", 64 * h, 64 * h + 64), a("P0R", h, 128, 2), 2.0 ** -11, OP.mult)
                ts(a("RL", 128 + 64 * h, 192 + 64 * h), a("X0R", h, 128, 2), XO, OP.add)
            t32(nd("C16", ALL, ALL), a("A16"))
            swap("C16")
            cp(chain(0), SD)

        def prep(r):
            for h in (1, 3, 0, 2):
                ts(a("PO", 32 * h, 32 * h + 32), chain(r, h, 128, 4), 2048.0, OP.mult)
            if SPREAD == "V":
                for l in range(2):
                    ts(nd("XQ", ALL, l, ALL), text(r), XO, OP.subtract)
                cp(nd("XQ", ALL, slice(2, 4), ALL), nd("XQ", ALL, slice(0, 2), ALL))
                cp(XR, nd("XQ", ALL, ALL, ALL))
            else:
                for l in range(4):
                    mm(nd("sp", slice(l, 32, 4), ALL), A("IDH"), text(r), l == 0, l == 3)
                if SPREAD == "S":
                    act(XR, nd("sp", ALL, ALL), bias=-XO)
                else:
                    ts(XR, nd("sp", ALL, ALL), XO, OP.subtract)
            tt(a("NE", 1, 64), chain(r, 0, 63), chain(r, 64, 127), OP.not_equal)
            for h in range(2):
                scan(a("RQ", 64 * h, 64 * h + 64), a("NE"), A("RES", 0, 64), OP.max, OP.min)
            mm(Z, A("IDH"), A("CF", 0, 128), True, False)
            mm(Z, A("ID"), A("KA"), False, False)
            mm(Z, A("IDH"), chain(r), False, True)

        def sums(e, ex, lin):
            out = a("k", e, 128, 2)
            mm(out, A("ID"), A(ex, e, 128, 2), True, False)
            for h in lin:
                for b in range(16):
                    mm(a("k", h, 128, 4), A("FN", 15 - b, 143 - b), a("DF", 512 * h + b, 512 * h + 512, 16), False, False)
            for b in list(range(0, 16, 2)) + list(range(1, 16, 2)):
                mm(out, A("FS", 15 - b, 143 - b), nd("AD", ALL, slice(e, 16, 2), b), False, b == 15)

        def dist(off, ex, who):
            bank = 0
            for h, q in zip((1, 3, 0, 2), who):
                o = a(off, 32 * h, 32 * h + 32)
                if q != "S":
                    src, lo = "DF", 512 * h
                    gat(a(src, lo, lo + 512), WIN, o, XR, OP.subtract)
                else:
                    src, lo = ("ta", "tb")[bank % 2], 0
                    bank += 1
                    act(a("TG", 512 * h, 512 * h + 512), WIN, AF.Copy, off=o)
                    mm(a(src), A("NID"), nd("XQ", ALL, ALL, ALL) if SPREAD == "V" else XR, True, False)
                    mm(a(src), A("ID"), a("TG", 512 * h, 512 * h + 512), False, True)
                if q == "R":
                    ts(nd("AD", ALL, slice(h, 16, 4), ALL), a(src, lo, lo + 512), 0.0, OP.max, 2.0, OP.mult)
                else:
                    st = 2 if h == 2 + PARITY[1] else 1
                    for b0 in range(st):
                        act(nd("AD", ALL, slice(h, 16, 4), slice(b0, 16, st)), a(src, lo + b0, lo + 512, st), AF.Abs)
            for e in PARITY:
                sums(e, ex, [h for h, q in zip((1, 3, 0, 2), who) if q == "R" and h % 2 == e])

        def charges(r):
            scan(a("FM"), a("RQ"), K, OP.mult, OP.max)
            tt(a("NR"), K, a("FM"), OP.not_equal)
            scan(a("LL", 0, 128), a("NR"), Z, OP.mult, OP.max)
            last = a("LL", 15, 128, 16)
            ts(small(0), last, M2, OP.add, M2, OP.subtract)
            ts(small(1), last, M32, OP.add, M32, OP.subtract)
            mps = nd("sp", slice(16, 20), ALL)
            for c in range(8):
                ou, ov = a("OU", 128 * c, 128 * c + 128), a("OV", 64 * c, 64 * c + 64)
                kk, hh = a("SM", c, c + 1), a("SM", 8 + c, 9 + c)
                ts(ou, A("IU"), kk, OP.add, hh, OP.is_equal)
                ts(ov, A("IV"), hh, OP.add, a("LL", 16 * c + 15, 16 * c + 16), OP.is_equal)
                mm(mps, ou, ov, c == 0, c == 7)
            ms = table(r, rank)
            ts(ms, mps, 0.5, OP.is_ge)
            send([(ms, ms, d, e) for d, e in spread_plan(core)], "mk%d_%d" % (s, r), [table(r, j) for j in range(NG) if j != rank],
                 sum(len(e) for c in T.cores if c != core for d, e in spread_plan(c) if core in d), TABLES)

        def teach(r):
            zk, zt = a("LL", 15, 128, 16), a("LL", 143, 256, 16)
            if r:
                act(a("SG"), K, AF.Sign, bias=0.5 - CUTKEY)
                mm(a("k", 256, 512), A("IDH"), A("CF"), True, False)
                mm(a("k", 256, 512), A("ID"), A("KG"), False, False)
                mm(a("k", 256, 384), A("IDH"), chain(r), False, False)
                mm(a("k", 385, 512), A("IDH"), chain(r, 0, 127), False, False)
                mm(a("k", 256, 384), A("ID64"), a("SG"), False, False)
                mm(a("k", 384, 512), A("ID64"), a("SG"), False, True)
            scan(a("LL", 129, 256), a("NR", 1, 128), a("k", 128, 255), OP.mult, OP.max)
            if r:
                scan(a("GL"), A("RES"), a("k", 256, 512), OP.mult, OP.max)
                tt(small(2, 2), a("GL", 15, 256, 16), a("LL", 15, 256, 16), OP.max)
                ts(small(7), a("FM", 15, 128, 16), CUTKEY, OP.min)
                ts(small(8), a("GL", 15, 128, 16), CUTKEY, OP.mult, CUTKEY, OP.min)
                tt(small(9), small(7), small(8), OP.max)
                zk, zt = small(2), small(3)
            kk = a("BKA", 0, 128, 16)
            ts(kk, zk, M2, OP.add, M2 + 32, OP.subtract)
            tt(small(5), zt, kk, OP.subtract)
            tt(small(4), zk, kk, OP.subtract)
            ts(a("TEO"), small(5), 2048.0, OP.mult, 2048 * (OFF - 34), OP.add)
            ts(small(6), small(4), OFF - 32, OP.add)
            gat(a("A16"), a("PU"), a("TEO"), 2.0 ** -11, OP.mult)
            t32(nd("C16", ALL, ALL), a("A16"))
            swap("C16")
            for h in (1, 3, 0, 2):
                ts(a("PD", 32 * h, 32 * h + 32), nd("sp", slice(0, 8), slice(h, 16, 4)), 2048.0, OP.mult)
            scan(a("OS"), A("RES", 0, 128), a("BKA"), OP.mult, OP.add)
            ts(a("OH"), a("OS"), 0.0, OP.is_equal)

        def cuts(r):
            mine = [q for q in range(4) if QUARTERS[q] == "S"]
            banks = [("ta", "tb", "k", "ta")[mine.index(q)] if q in mine else "k" for q in range(4)]
            if len(mine) == 3:
                banks[mine[2]] = "ta"
            for q in mine[:2]:
                mm(a(banks[q]), A("ID"), a("TX", 512 * q, 512 * q + 512), True, False)
            sm, ct = a("k", 256, 320), a("CT", 64 * r, 64 * r + 64)
            js = [rank] + [j for j in range(NG) if j != rank]
            for j in js:
                mm(sm, A("ID"), table(r, j), j == js[0], j == js[-1])
            act(ct, sm, AF.Relu, bias=-3.0)
            for q in range(4):
                tx, b = a("TX", 512 * q, 512 * q + 512), a(banks[q])
                if q in mine[2:]:
                    mm(b, A("ID"), tx, True, False)
                for u in range(8):
                    v = 8 * q + u
                    j = mm(a(banks[q], 64 * u, 64 * u + 64), A("REP", 128 * v, 128 * v + 128), ct, u == 0 and QUARTERS[q] == "V", u == 7,
                           (j, 0.0) if v else None)
                if QUARTERS[q] == "S":
                    act(tx, b, AF.Copy)
                else:
                    tt(tx, b, tx, OP.add)
            if r == NR - 1:
                o = nd("sp", slice(20, 24), ALL)
                for j in range(NR):
                    mm(o, A("ID"), a("CT", 64 * j, 64 * j + 64), j == 0, j == NR - 1)
                act(a("YC"), o, AF.Sign)
                put("Y", lambda: g.sync.dma_start(T.yc[4 * s:4 * s + 4, :], a("YC")[0]).then_inc(T.sem["oyc%d" % s], 16), [], [a("YC")], 0.05, ("", 0))

        def replace(r):
            last, NB, NV = a("L3", 15, 128, 16), a("k", 256, 384), a("k", 384, 512)
            xd, x, tk, of, n1 = [small(j) for j in range(10, 15)]
            scan(a("F3"), A("RESB"), K, OP.add, OP.min)
            tt(a("NR"), K, a("F3"), OP.not_equal)
            tt(xd, a("F3", 15, 128, 16), small(9) if r else a("FM", 15, 128, 16), OP.subtract)
            tt(a("D1"), SD, a("NR"), OP.subtract)
            tt(x, xd, A("BASE"), OP.min)
            scan(a("L3"), a("NR"), a("D1"), OP.mult, OP.max)
            ts(tk, xd, 0.0, OP.is_le)
            tt(of, x, last, OP.max)
            tt(n1, last, small(6), OP.subtract)
            ts(a("OFO"), of, 2048.0, OP.mult)
            tt(a("BKB", 0, 128, 16), n1, tk, OP.mult)
            gat(a("SU"), a("TX"), a("OFO"), text(r), OP.add)
            scan(NB, A("RES", 0, 128), a("BKB"), OP.mult, OP.add)
            ps, xs = a("RS", 256 * r, 256 * r + 128), a("RS", 256 * r + 128, 256 * r + 256)
            ts(xs, a("SU"), 0.5, OP.mult, XO / 2 - 0.25, OP.add)
            tt(NV, NB, a("OH"), OP.mult)
            if r + 1 < NR:
                tt(ps, NV, chain(r), OP.add)
                there = chain(r + 1, 0, 256)
                send([(a("RS", 256 * r, 256 * r + 256), there, [nxt], pow2(common(core, [nxt])))], "rg%d_%d" % (s, r + 1),
                     [there], len(pow2(common(prv, [core]))), RING)
            else:
                tt(nd("PN", ALL, ALL), NV, chain(r), OP.add)
                swap("PN")
                for h in range(2):
                    ts(a("YX", h, 128, 2), a("RS", 256 * r + 128 + 64 * h, 256 * r + 192 + 64 * h), XO, OP.subtract)
                store("SS", T.yx, "YX%d" % s, s, "oyx%d" % s)
                t32(a("YPA"), SD)
                for h in range(2):
                    ts(a("YP", h, 128, 2), a("YPA", 64 * h, 64 * h + 64), 2048.0, OP.mult)
                store("YS", T.yp, "YP%d" % s, s, "oyp%d" % s)

        first()
        for r in range(NR):
            prep(r)
            dist("PO", "EX1", CHAINS)
            charges(r)
            teach(r)
            cuts(r)
            dist("PD", "EX2", PUPILS)
            replace(r)

    for s in range(2):
        now[0] = s
        one_set(s)
    cnt = issue()

    for s in STORES + LOADS:
        g.sync.wait_ge(T.sem[s], 16 if s[1:3] == "yc" else 32)
    g.wait_ge(T.sem.loc, sent[0])
    for q in ("V", "S", "P", "G"):
        g.wait_ge(T.sem[SEM[q]], cnt[q])
